import numpy as np, ml_dtypes
CORES = [9,25,41,57]
N = 4
BF = ml_dtypes.bfloat16
V, HV, LV, K, T, S, EPS, LK = 4096, 2048, 12, 256, 5, 1, 72, 9
def pick(tab, ix):
    return np.take_along_axis(tab, ix[:, :, None, :], 3)
def parts(rng):
    px = np.clip(rng.integers(0, 256, (1, 8, 16, V)) + rng.integers(-48, 49, (N, 8, 16, V)), 0, 255)
    vi = rng.integers(0, V, (N, 8, 16, V))
    few = rng.integers(0, V, (N, 8, 16))
    v = np.where(rng.random((N, 8, K)) < 0.25, np.take_along_axis(few, rng.integers(0, 16, (N, 8, K)), 2), rng.integers(0, V, (N, 8, K)))
    near = np.clip(pick(px, v) + rng.integers(-120, 121, (N, 8, 16, K)), 0, 255)
    z = np.where(rng.random((N, 8, 1, K)) < 0.4, near, rng.integers(0, 256, (N, 8, 16, K)))
    f = rng.integers(0, V, (N, 8, 16, K)); d = rng.integers(0, 4, (N, 8, K))
    return px, vi, z, f, v, d, rng.integers(0, 256, (N, 8, 16)), rng.integers(0, 4096, (N, 8, 16))
def pack(px, vi, z, f, v, d, w, k):
    return {"px": np.ascontiguousarray(px.reshape(N, 128, V)).astype(np.float32).astype(BF), "vw": (vi[..., :HV] + V * vi[..., HV:]).reshape(N, 128, HV).astype(np.int32),
            "z0": z.reshape(N, 128, K).astype(np.float32).astype(BF), "f0": f.reshape(N, 128, K).astype(np.int32), "v0": v.astype(np.int32), "d0": d.astype(np.int32),
            "wt": w.reshape(N, 128, 1).astype(np.int32), "kap": k.reshape(N, 128, 1).astype(np.int32)}
def setup_inputs(rng):
    return pack(*parts(rng))
def setup_inputs_corners(rng):
    px, vi, z, f, v, d, w, k = parts(rng); own = np.arange(V)[None, :]; lane = np.arange(16); i = np.arange(K); one = 0 * i
    for r in range(N):
        for g in range(8):
            m = r + g
            d[r, g] = (one, one + 1, one + 3, 3 * (i & 1))[m & 3]
            v[r, g] = (one + (0, V - 1, HV)[m % 3], rng.permutation(V)[:K], (V - 1) * (i & 1), V - K + i)[(r + (g >> 1)) & 3]
            vi[r, g] = (own + 0 * lane[:, None], V - 1 - own + 0 * lane[:, None], (own + 1 + lane[:, None]) & (V - 1), (V - 1) * rng.integers(0, 2, (16, V)))[g & 3]
            f[r, g] = vi[r, g][:, v[r, g]] if m & 1 else (V - 1) * rng.integers(0, 2, (16, K))
            w[r, g] = (0 * lane, 0 * lane + 255, 255 * (lane == 15), w[r, g])[(m >> 1) & 3]
            k[r, g] = (0 * lane, 0 * lane + 4095, 4095 * (lane == 15), k[r, g])[(r + 3 * g) & 3]
            likes = (i >= 0, i < 0, (i & 1) == 0, (i & 1) == 1, rng.random(K) < 0.5)[(r + 2 * g) % 5]
            x = px[r, g][:, v[r, g]]; z[r, g] = np.where(likes[None, :], x, (x + 128) & 255)
    return pack(px, vi, z, f, v, d, w, k)
def setup_inputs_ends(rng):
    def bits(*shape):
        return rng.integers(0, 2, shape)
    pat = 255 * bits(N, 8, 16, 6); pat[..., 0] = 0; pat[..., 1] = 255; pat[..., 3] = 255 - pat[..., 2]
    px = np.take_along_axis(pat, rng.integers(0, 6, (N, 8, 1, V)), 3)
    px[..., 0] = 0; px[..., V - 1] = 255; px[..., V - 613] = 255
    vi = (V - 1) * bits(N, 8, 16, HV); vi = np.concatenate([vi, vi], axis=3)
    z = 255 * bits(N, 8, 16, K); f = (V - 1) * bits(N, 8, 16, K); v = (V - 1) * bits(N, 8, K); d = 3 * bits(N, 8, K)
    w = 255 * bits(N, 8, 16); w[:, 1::2] = 255; k = 4095 * bits(N, 8, 16); k[..., 15] = 4095
    for h in (0, K - 4):
        z[..., h] = 255; v[..., h] = V - 1
        z[..., h + 1] = 255; v[..., h + 1] = 0; d[..., h + 1] = 3
        z[..., h + 2] = 0; z[:, :, 0, h + 2] = 255; z[:, :, 1, h + 2] = 2; v[..., h + 2] = V - 1
        z[..., h + 3] = 0; v[..., h + 3] = V - 1
    return pack(px, vi, z, f, v, d, w, k)
def setup_inputs_spread(rng):
    px = np.minimum((np.exp2(8 * rng.random((N, 8, 1, V))) * rng.random((N, 8, 16, V))).astype(np.int64), 255)
    z = np.minimum((np.exp2(8 * rng.random((N, 8, 1, K))) * rng.random((N, 8, 16, K))).astype(np.int64), 255)
    vi = np.minimum((V * rng.random((N, 8, 16, V)) ** 3).astype(np.int64), V - 1)
    f = np.minimum((V * rng.random((N, 8, 16, K)) ** 4).astype(np.int64), V - 1)
    v = np.minimum((V * rng.random((N, 8, K)) ** 2).astype(np.int64), V - 1)
    d = np.minimum((4 * rng.random((N, 8, K)) ** 2).astype(np.int64), 3)
    w = np.minimum(np.exp2(8 * rng.random((N, 8, 16))).astype(np.int64), 255); k = np.minimum(np.exp2(12 * rng.random((N, 8, 16))).astype(np.int64), 4095)
    return pack(px, vi, z, f, v, d, w, k)
def setup_inputs_ties(rng):
    px, vi, z, f, v, d, w, k = parts(rng)
    pat = np.broadcast_to(rng.integers(0, 256, (1, 8, 16, 8)), (N, 8, 16, 8))
    px = np.take_along_axis(pat, rng.integers(0, 8, (N, 8, 1, V)), 3)
    v = np.take_along_axis(rng.integers(0, V, (N, 8, 24)), rng.integers(0, 24, (N, 8, K)), 2)
    x = pick(px, v); n = LK - rng.integers(0, 2, (N, 8, 1, K)); o = np.argsort(rng.random((N, 8, 16, K)), axis=2)
    far = EPS + (o >= n).astype(np.int64); z = np.where(x + far <= 255, x + far, x - far)
    vi = np.where(rng.random((N, 8, 16, V)) < 0.2, np.arange(V), vi)
    return pack(px, vi, z, f, v, d, w, k)
def check_inputs(d):
    bad = []
    for a, lo, hi in (("px", 0, 255), ("vw", 0, V * V - 1), ("z0", 0, 255), ("f0", 0, V - 1), ("v0", 0, V - 1), ("d0", 0, 3), ("wt", 0, 255), ("kap", 0, 4095)):
        x = np.asarray(d[a]).astype(np.float64)
        if not (np.min(x) >= lo and np.max(x) <= hi): bad.append("range of " + a)
        if not np.all(x == np.rint(x)): bad.append("whole numbers of " + a)
    return bad
def distances(X, ix, q):
    flat = ix.reshape(N, 8, 16 * K); out = np.zeros((N, 8, 16, K), np.int64)
    for i in range(16):
        out += np.abs(np.take_along_axis(X[:, :, i], flat, 2).reshape(N, 8, 16, K) - q[:, :, i][:, :, None, :])
    return out
def place(view, k):
    return np.take_along_axis(view, k[:, :, None, :], 2)[:, :, 0]
def reference(px, vw, z0, f0, v0, d0, wt, kap):
    X = px.astype(np.int64).reshape(N, 8, 16, V); packed = vw.astype(np.int64).reshape(N, 8, 16, HV)
    vi = np.concatenate([packed & (V - 1), packed >> LV], axis=3)
    z = z0.astype(np.int64).reshape(N, 8, 16, K); f = f0.astype(np.int64).reshape(N, 8, 16, K); v = v0.astype(np.int64); dl = d0.astype(np.int64); A = np.zeros((N, 8, K), np.int64)
    wl = wt.astype(np.int64).reshape(N, 8, 16, 1); kl = kap.astype(np.int64).reshape(N, 8, 16, 1); other = np.arange(K) ^ 1
    for t in range(T):
        x = pick(X, v); e = pick(vi, v)
        like = np.add.reduce((np.abs(x - z) <= EPS).astype(np.int64), axis=2) >= LK + (A & 1); L = like[:, :, None, :]
        u = np.add.reduce(wl * z, axis=2) & (V - 1)
        h = np.where(L, f, (((u[:, :, None, :] * kl) >> 5) + 613 * v[:, :, None, :]) & (V - 1))
        de = distances(X, e, x); dh = distances(X, h, np.where(L, x, z))
        e = np.where(L & (dh < de), h, e)
        for r in range(N):
            for g in range(8):
                j = np.flatnonzero(like[r, g]); users, first = np.unique(v[r, g, j], return_index=True)
                vi[r, g][:, users] = e[r, g][:, j[first]]
        z = np.where(L, (z + x) >> 1, z); A = A + like.astype(np.int64); dl = np.where(like, 0, dl + 1)
        s = np.add.reduce(z, axis=2)
        v = np.where(like, place(e, (s + t) & 15), place(h, np.argmin(dh, axis=2)))
        f = e; second = place(e, (s + t + 8) & 15)
        over = like[:, :, other] & (dl >= 2); O = over[:, :, None, :]
        z = np.where(O, z[..., other], z); f = np.where(O, f[..., other], f); A = np.where(over, A[..., other], A)
        v = np.where(over, second[..., other], v); dl = np.where(over, 0, dl)
        if t < T - 1: z, f, v, A, dl = [np.roll(a, S, axis=0) for a in (z, f, v, A, dl)]
    return {"yw": (vi[..., :HV] + V * vi[..., HV:]).reshape(N, 128, HV).astype(np.float32), "yz": z.reshape(N, 128, K).astype(np.float32), "yf": f.reshape(N, 128, K).astype(np.float32),
            "yv": v.astype(np.float32), "yc": (16 * A + dl).astype(np.float32)}

@@ -1,0 +1,720 @@
+import numpy as np
+from concourse.bass import DstId, RemoteDMATransfer
+from concourse.mybir import dt, AluOpType, AxisListType, ActivationFunctionType
+
+A = AluOpType
+F = ActivationFunctionType
+n = 128
+NT = 5
+XW = 32 + 3 * n
+WW = 4 * n
+MAGIC = 12582912.0
+BIAS = 10.0
+NE = 64
+f4, b2, h2, i4, u2 = "float32", "bfloat16", "float16", "int32", "uint16"
+
+SCRATCH = {
+    "PX": ("sbuf", [128, 4096], b2), "VI": ("sbuf", [128, 4096 + 2 * n], f4), "VW": ("sbuf", [128, 2048], i4),
+    "IT": ("sbuf", [128, 1024], i4), "YT": ("sbuf", [128, 2048], f4), "YU": ("sbuf", [128, 2048], f4),
+    "XZ": ("sbuf", [128, 10 * XW], b2), "W": ("sbuf", [128, 10 * WW], f4), "VH": ("sbuf", [128, 10 * 8], h2),
+    "ZB": ("sbuf", [128, 10 * (32 + n)], b2), "FB": ("sbuf", [128, 10 * n], f4), "VB": ("sbuf", [128, 10 * 8], h2),
+    "HE": ("sbuf", [128, 4 * n], f4), "HEL": ("sbuf", [128, 4 * n], u2), "QS": ("sbuf", [128, 16 * n], h2), "QX": ("sbuf", [128, 32 * n], h2),
+    "GH": ("sbuf", [128, 32 * n], b2), "GE": ("sbuf", [128, 32 * n], b2), "DH": ("sbuf", [128, 32 * n], h2), "DE": ("sbuf", [128, 32 * n], h2),
+    "RH": ("sbuf", [128, 32 * n], h2), "RE": ("sbuf", [128, 32 * n], h2),
+    "OTL": ("sbuf", [128, 16], u2), "AB": ("sbuf", [128, 2 * n], b2), "IND": ("sbuf", [128, 2 * n], h2), "LK": ("sbuf", [128, 16], h2),
+    "LSL": ("sbuf", [128, 32], u2), "HI1": ("sbuf", [128, 2 * n], i4), "HI2": ("sbuf", [128, 2 * n], i4), "T1": ("sbuf", [128, 2 * n], f4),
+    "D1": ("sbuf", [128, 16], b2), "OV": ("sbuf", [128, 16], h2), "TLL": ("sbuf", [128, 48], u2), "P1": ("sbuf", [128, 16], b2), "RA": ("sbuf", [128, 80], b2),
+    "KI": ("sbuf", [128, 2 * n], i4), "KJ": ("sbuf", [128, 2 * n], i4), "CB": ("sbuf", [128, 16], b2), "SJb": ("sbuf", [128, 2048], b2), "OK": ("sbuf", [128, 16], f4), "CLB": ("sbuf", [128, 8], f4), "OHL": ("sbuf", [128, 2 * n], b2), "RL": ("sbuf", [128, 2 * n], b2),
+    "VS": ("sbuf", [128, 2 * n], f4), "VR": ("sbuf", [128, 2 * n], f4), "EQ": ("sbuf", [128, 2 * n], b2),
+    "W0": ("sbuf", [128, 16], h2), "O2": ("sbuf", [128, 16], f4), "OFF": ("sbuf", [128, 32], u2),
+    "HME": ("sbuf", [128, 2 * n], f4), "KEY": ("sbuf", [128, 2 * n], f4), "MT": ("sbuf", [128, 2 * n], b2), "MM": ("sbuf", [128, 2 * n], f4),
+    "PM": ("sbuf", [128, 2 * n], f4), "MN": ("sbuf", [128, 2 * n], f4), "OHT": ("sbuf", [128, 2 * n], b2), "CF": ("sbuf", [128, 2 * n], f4), "PP": ("sbuf", [128, 2 * n], h2),
+    "I16b": ("sbuf", [128, 128], b2), "I8184": ("sbuf", [128, 128], h2), "I8k": ("sbuf", [128, 128], h2), "I8kn": ("sbuf", [128, 128], h2), "BO613": ("sbuf", [128, 128], h2), "C256": ("sbuf", [128, n], h2),
+    "If": ("sbuf", [128, 128], f4), "Ib": ("sbuf", [128, 128], b2), "Ih": ("sbuf", [128, 128], h2), "Inb": ("sbuf", [128, 128], b2), "Ihalf": ("sbuf", [128, 128], b2),
+    "Sb": ("sbuf", [128, 128], b2), "Sh": ("sbuf", [128, 128], h2), "Sh100": ("sbuf", [128, 128], h2), "In": ("sbuf", [128, 128], h2), "I2n": ("sbuf", [128, 128], h2),
+    "Ip100": ("sbuf", [128, 128], h2), "Im100": ("sbuf", [128, 128], h2), "I8": ("sbuf", [128, 128], h2),
+    "G2n": ("sbuf", [128, 128], h2), "Gn": ("sbuf", [128, 128], h2), "G0": ("sbuf", [128, 128], h2),
+    "ONE": ("sbuf", [128, 128], f4), "G8": ("sbuf", [128, 128], f4), "BO": ("sbuf", [128, 128], b2), "BOn": ("sbuf", [128, 128], b2), "BOh": ("sbuf", [128, 128], h2), "BOg": ("sbuf", [128, 128], b2), "WB": ("sbuf", [128, 128], b2),
+    "Bh": ("sbuf", [128, 144], h2), "B32": ("sbuf", [128, 8], h2), "Bm16": ("sbuf", [128, 8], h2),
+    "SJ": ("sbuf", [128, 2048], h2), "LTJ": ("sbuf", [128, 2048], b2), "PI": ("sbuf", [128, 32], i4), "PC": ("sbuf", [128, 16], f4),
+    "OJ": ("sbuf", [128, 16], f4),  "IJ": ("sbuf", [128, 16], f4), "CMI": ("sbuf", [128, 8], f4), "CM": ("sbuf", [128, 24], h2), "CMm": ("sbuf", [128, 16], h2),
+    "CON": ("sbuf", [128, 64], h2), "KC": ("sbuf", [128, 128], b2), "MK": ("sbuf", [128, 16 * n], h2), "MF": ("sbuf", [128, n], f4), "RST": ("sbuf", [128, 128], f4),
+    "CQ": ("sbuf", [128, 128], b2), "ON": ("sbuf", [128, 128], b2), "WT": ("sbuf", [128, 2], i4), "WTf": ("sbuf", [128, 8], f4),
+    "VZ": ("sbuf", [128, 512], i4), "VZi": ("sbuf", [128, 512], i4), "VZh": ("sbuf", [128, 768], h2), "FI": ("sbuf", [128, 256], i4), "YC": ("sbuf", [128, 16], h2), "YI": ("sbuf", [128, 2 * n], i4),
+}
+for _b in range(8):
+    SCRATCH["b%d" % _b] = ("psum", [128, 512], f4)
+LOADS = ["px0", "px1", "vw0", "vw1", "z0", "z1", "f0", "v0", "d0", "wt", "kap"]
+SEMAPHORES = ["V", "S", "P", "G", "out", "ls"] + ["ld_" + x for x in LOADS] + ["r%s_%d_%d" % (k, t, h) for k in "zfv" for t in range(1, NT) for h in range(2)]
+
+
+def ref(name, c0, c1, step=1, p0=0, p1=128, pstep=1):
+    return (name, c0, c1, step, p0, p1, pstep)
+
+
+def new_prog():
+    return {"ops": [], "acc": {}, "rr": [0, 0], "st": 0.0}
+
+
+def touch(pg, o, r, wr):
+    name, c0, c1 = r[0], r[1], r[2]
+    lst = pg["acc"].setdefault(name, [])
+    psum = name[0] == "b" and name[1:].isdigit()
+    ops = pg["ops"]
+    keep = []
+    for a in lst:
+        p, a0, a1, aw = a
+        over = a0 < c1 and c0 < a1
+        if p != o["i"]:
+            if psum:
+                if ops[p]["q"] != o["q"]:
+                    o["dep"].add(p)
+                elif over and (wr or aw) and not (ops[p]["q"] == "P"):
+                    o["dep"].add(p)
+            elif over and (wr or aw):
+                if aw or ops[p]["q"] != o["q"]:
+                    o["dep"].add(p)
+                else:
+                    o["ord"].add(p)
+        if wr and a0 >= c0 and a1 <= c1 and p != o["i"] and not psum and r[3] == 1 and r[6] == 1:
+            continue
+        keep.append(a)
+    if psum and len(keep) > 24:
+        keep = keep[-24:]
+    keep.append((o["i"], c0, c1, wr))
+    pg["acc"][name] = keep
+
+
+def add(pg, q, cost, fn, rd, wr, sem=None, val=1, after=(), lat=0.0, tag=""):
+    o = {"i": len(pg["ops"]), "q": q, "cost": cost, "fn": fn, "dep": set(after), "ord": set(), "sem": sem, "val": val, "lat": lat, "send": None, "tag": tag, "st": pg["st"]}
+    pg["ops"].append(o)
+    for r in rd:
+        touch(pg, o, r, False)
+    for r in wr:
+        touch(pg, o, r, True)
+    return o["i"]
+
+
+WAKE = 0.10
+FIX = {"V": 0.03, "S": 0.04, "P": 0.03, "G": 0.05, "Y": 0.05}
+
+
+def schedule(pg):
+    ops = pg["ops"]
+    N_ = len(ops)
+    succ = [[] for _ in ops]
+    cnt = [0] * N_
+    for o in ops:
+        ps = set(o["dep"]) | o["ord"]
+        if o["send"] is not None:
+            ps.add(o["send"])
+        cnt[o["i"]] = len(ps)
+        for p in ps:
+            succ[p].append(o["i"])
+    pri = [0.0] * N_
+    for o in reversed(ops):
+        i = o["i"]
+        pri[i] = max([pri[s] for s in succ[i]] + [0.0]) + o["cost"] + o["lat"] + WAKE
+    for o in ops:
+        pri[o["i"]] += o["st"]
+    ready = {}
+    avail = [0.0] * N_
+    free = {}
+    order = {}
+    fin = [0.0] * N_
+    for o in ops:
+        if cnt[o["i"]] == 0:
+            ready.setdefault(o["q"], []).append(o["i"])
+    left = N_
+    while left:
+        best = None
+        for q, lst in ready.items():
+            if not lst:
+                continue
+            if q[0] == "R":
+                cand = (avail[lst[0]], q, lst[0])
+            else:
+                fr = free.get(q, 0.0)
+                st = min(max(fr, avail[i]) for i in lst)
+                c = [i for i in lst if max(fr, avail[i]) <= st + 0.02]
+                cand = (st, q, max(c, key=lambda i: pri[i]))
+            if best is None or cand[0] < best[0]:
+                best = cand
+        st, q, i = best
+        ready[q].remove(i)
+        o = ops[i]
+        end = st + o["cost"]
+        free[q] = end
+        fin[i] = end + o["lat"]
+        order.setdefault(q, []).append(i)
+        left -= 1
+        for s in succ[i]:
+            cnt[s] -= 1
+            w = 0.0 if i in ops[s]["ord"] else WAKE
+            avail[s] = max(avail[s], fin[i] + w)
+            if cnt[s] == 0:
+                ready.setdefault(ops[s]["q"], []).append(s)
+        o["t0"], o["t1"] = st, end
+    pg["order"] = order
+    pg["fin"] = max(fin)
+    pg["seq"] = sorted(range(N_), key=lambda i: (ops[i]["t0"], ops[i]["q"][0] != "R", i))
+
+
+def emit(pg, g, T):
+    ops = pg["ops"]
+    eng = {"V": g.vector, "S": g.scalar, "P": g.tensor, "G": g, "Y": g.sync}
+    pos, key, know = {}, {}, {}
+    for q, lst in pg["order"].items():
+        c = 0
+        for i in lst:
+            if ops[i]["sem"] is None:
+                c += 1
+                key[i], pos[i] = q, c
+            else:
+                key[i], pos[i] = ops[i]["sem"], ops[i]["val"]
+    qk = {}
+    done = {}
+    queues = {q: list(l) for q, l in pg["order"].items()}
+    state = {q: 0 for q in queues}
+    prog = True
+    tot = sum(len(l) for l in queues.values())
+    k = 0
+    while k < tot:
+        prog = False
+        for q in queues:
+            while state[q] < len(queues[q]):
+                i = queues[q][state[q]]
+                o = ops[i]
+                if any(d not in done for d in o["dep"]) or (o["send"] is not None and o["send"] not in done):
+                    break
+                kn = qk.setdefault(q, {})
+                if q[0] != "R":
+                    need = {}
+                    for d in sorted(o["dep"], key=lambda d: -ops[d]["t1"]):
+                        if kn.get(key[d], 0) >= pos[d]:
+                            continue
+                        if need.get(key[d], 0) < pos[d]:
+                            need[key[d]] = pos[d]
+                    ds = [d for d in o["dep"] if need.get(key[d], 0) == pos[d]]
+                    for d in ds:
+                        for d2 in ds:
+                            if d2 != d and key[d] in need and key[d2] in need and key[d] != key[d2] and know[d2].get(key[d], 0) >= pos[d]:
+                                need.pop(key[d])
+                    for kk in sorted(need):
+                        eng[q].wait_ge(T.sem[kk], int(need[kk]))
+                    for d in o["dep"]:
+                        for kk, v in know[d].items():
+                            if kn.get(kk, 0) < v:
+                                kn[kk] = v
+                    ins = o["fn"](eng[q])
+                    if o["sem"] is None:
+                        ins.then_inc(T.sem[q], 1)
+                me = dict(kn)
+                if o["send"] is not None:
+                    me = dict(know[o["send"]])
+                    for kk in list(me):
+                        me.pop(kk)
+                me[key[i]] = max(me.get(key[i], 0), pos[i])
+                know[i] = me
+                done[i] = 1
+                state[q] += 1
+                k += 1
+                prog = True
+        if not prog:
+            raise ValueError("no order")
+    for q in "VSPG":
+        if pg["order"].get(q):
+            c = sum(1 for i in pg["order"][q] if ops[i]["sem"] is None)
+            if c:
+                g.wait_ge(T.sem[q], int(c))
+
+
+def build(T, topo, core, rank):
+    pg = new_prog()
+    CY = 0.00083
+    GC = 1.5
+
+    def ap(r):
+        name, c0, c1, step, p0, p1, ps = r
+        t = T[name]
+        rows = slice(p0, p1) if ps == 1 else slice(p0, p1, ps)
+        cols = slice(c0, c1) if step == 1 else slice(c0, c1, step)
+        return t[rows, cols]
+
+    def cnt(r):
+        return (r[2] - r[1] + r[3] - 1) // r[3]
+
+    def two(*rs):
+        return all(SCRATCH[r[0]][2] in (b2, h2, u2) for r in rs)
+
+    def inap(x):
+        if x[0] == "ind":
+            return ap(x[1]).indirect(ap(x[2]))
+        return ap(x)
+
+    def regs(x):
+        return [x[1], x[2]] if x[0] == "ind" else [x]
+
+    def dcol(s):
+        return ap(s) if isinstance(s, tuple) else s
+
+    def vcost(e, c, ind):
+        return FIX["V"] + CY * max(64, e * (GC if ind else c)) + (0.03 if ind else 0)
+
+    def ts(out, in0, s1, op0, s2=None, op1=None):
+        ind = in0[0] == "ind"
+        sc = [s for s in (s1, s2) if isinstance(s, tuple)]
+        c = 0.5 if (not ind and two(out, in0)) else 1
+        if op1 is None:
+            fn = lambda e: e.tensor_scalar(ap(out), inap(in0), dcol(s1), None, op0)
+        else:
+            fn = lambda e: e.tensor_scalar(ap(out), inap(in0), dcol(s1), dcol(s2), op0, op1)
+        return add(pg, "V", vcost(cnt(out), c, ind), fn, regs(in0) + sc, [out], tag="ts " + out[0])
+
+    def tt(out, a, b, op):
+        ind = a[0] == "ind"
+        ps = any(r[0][0] == "b" and r[0][1:].isdigit() for r in (a, b) if r[0] != "ind")
+        return add(pg, "V", vcost(cnt(out), 1 if ps else 2, ind), lambda e: e.tensor_tensor(ap(out), inap(a), ap(b), op), regs(a) + [b], [out], tag="tt " + out[0])
+
+    def cp(out, a):
+        ind = a[0] == "ind"
+        return add(pg, "V", vcost(cnt(out), 0.5 if (not ind and two(out, a)) else 1, ind), lambda e: e.tensor_copy(ap(out), inap(a)), regs(a), [out], tag="cp " + out[0])
+
+    def scan(out, d0, d1, init, op0, op1):
+        return add(pg, "V", vcost(cnt(out), 0.5 if two(out, d0, d1) else 1, False), lambda e: e.tensor_tensor_scan(ap(out), ap(d0), ap(d1), init, op0, op1), [d0, d1], [out], tag="scan " + out[0])
+
+    def fill(out, c):
+        return add(pg, "V", vcost(cnt(out), 0.5 if two(out) else 1, False), lambda e: e.memset(ap(out), c), [], [out], tag="fill " + out[0])
+
+    def act(out, in_, func, bias=0.0, scale=1.0):
+        ind = in_[0] == "ind"
+        sc = [s for s in (bias, scale) if isinstance(s, tuple)]
+        return add(pg, "S", FIX["S"] + CY * max(64, cnt(out) * (GC if ind else 1)) + (0.04 if ind else 0),
+                   lambda e: e.activation(ap(out), inap(in_), func, bias=dcol(bias), scale=dcol(scale)), regs(in_) + sc, [out], tag="act " + out[0])
+
+    def pe(mms):
+        cost = 0.0
+        rd, wr = {}, {}
+        for out, l, r, s, e_ in mms:
+            k = 4 if SCRATCH[l[0]][2] == f4 else 1
+            cost += 0.00055 * k * max(min(64, cnt(l)), cnt(r)) + 0.006
+            for x in (l, r):
+                y = rd.get(x[0])
+                rd[x[0]] = (x[0], min(x[1], y[1]) if y else x[1], max(x[2], y[2]) if y else x[2], 1, 0, 128, 1)
+            y = wr.get(out[0])
+            wr[out[0]] = (out[0], min(out[1], y[1]) if y else out[1], max(out[2], y[2]) if y else out[2], 1, 0, 128, 1)
+
+        def fn(e):
+            ins = None
+            for out, l, r, s, e_ in mms:
+                ins = e.matmul(ap(out), ap(l), ap(r), s, e_)
+            return ins
+        return add(pg, "P", cost + FIX["P"], fn, list(rd.values()), list(wr.values()), tag="pe " + mms[0][0][0])
+
+    def acc(out, *pairs):
+        return [(out, l, r, i == 0, i == len(pairs) - 1) for i, (l, r) in enumerate(pairs)]
+
+    def bank(h, w=n):
+        b = 4 * h + pg["rr"][h] % 4
+        pg["rr"][h] += 1
+        return "b%d" % b
+
+    def load(name, out, src, q="Y"):
+        s = "ld_" + name
+        return add(pg, q, 0.1, lambda e: e.dma_start(ap(out), src).then_inc(T.sem[s], 16), [], [out], sem=s, val=16, lat=3.0, tag="load " + name)
+
+    nout = [0]
+
+    def store(dst, in_, q="Y"):
+        nout[0] += 16
+        return add(pg, q, 0.1, lambda e: e.dma_start(dst, ap(in_)).then_inc(T.sem["out"], 16), [in_], [], sem="out", val=nout[0], lat=2.5, tag="store")
+
+    dst = T.cores[(rank + 1) % 4]
+    rid, pid, _se = topo.addr(dst)
+    mask = sum(1 << e for e in topo.engines(core, dst))
+    neng = len(topo.engines(core, dst))
+    nls = [0]
+
+    def send(kind, t, h, out, in_):
+        s = "r%s_%d_%d" % (kind, t, h)
+        nls[0] += neng
+        i = add(pg, "G", 0.4, lambda e: e.remote_dma(ap(out), ap(in_), T.sem[s], T.sem["ls"], pid, rid, mask), [in_], [], sem="ls", val=nls[0], lat=1.6, tag="send " + s)
+        j = add(pg, "R" + s, 0.0, None, [], [out], sem=s, val=neng)
+        pg["ops"][j]["send"] = i
+
+    sm = lambda name, h, w=8, x=0, k=8: ref(name, h * w + x, h * w + x + k)
+    tl = lambda name, h: ref(name, h * n, h * n + n)
+    full = lambda name: ref(name, 0, SCRATCH[name][1][1])
+
+    load("wt", ref("WT", 0, 1), T.wt[:, :])
+    load("kap", ref("WT", 1, 2), T.kap[:, :])
+    fill(full("VZ"), 0)
+    load("v0", ref("VZ", 0, 256, 1, 0, 128, 16), T.v0[:, :])
+    load("d0", ref("VZ", 256, 512, 1, 0, 128, 16), T.d0[:, :])
+    load("px0", ref("PX", 0, 2048), T.px[:, 0:2048])
+    load("px1", ref("PX", 2048, 4096), T.px[:, 2048:4096])
+    for h in (1, 0):
+        load("z%d" % h, ref("XZ", h * XW + 32, h * XW + 32 + n), T.z0[:, h * n:h * n + n])
+    load("f0", full("FI"), T.f0[:, :])
+    load("vw0", ref("VW", 0, 1024), T.vw[:, 0:1024])
+    load("vw1", ref("VW", 1024, 2048), T.vw[:, 1024:2048])
+
+    def sel(out, in_, pat, cmp, fillv, base, cm):
+        return add(pg, "G", 0.2 + 2 * CY * cnt(out), lambda e: e.affine_select(ap(out), ap(in_), pat, cmp, fillv, base, cm), [in_], [out], tag="sel")
+
+    def iota(out, pat, base, cm, small=False):
+        if small:
+            fn = lambda e: e.iota(ap(out), pat, base, cm, allow_small_or_imprecise_dtypes=True)
+        else:
+            fn = lambda e: e.iota(ap(out), pat, base, cm)
+        return add(pg, "G", 0.2 + 2 * CY * cnt(out), fn, [], [out], tag="iota")
+
+    fill(full("ONE"), 1.0)
+    sel(full("G8"), full("ONE"), [[1, 128]], A.is_ge, 0.0, 0, -16)
+    sel(full("G8"), full("G8"), [[-1, 128]], A.is_ge, 0.0, 15, 16)
+    sel(full("If"), full("ONE"), [[-1, 128]], A.is_equal, 0.0, 0, 1)
+    iota(ref("PI", 0, 1), [[0, 1]], 0, 1)
+    iota(full("IJ"), [[1, 16]], 0, 0, True)
+    iota(full("CMI"), [[16, 8]], 0, 0, True)
+    iota(full("KC"), [[0, 8], [1, 16]], 0, 0, True)
+    g8 = ref("G8", 0, 128, 1, 0, 8)
+    bk = "b7"
+    pe([(ref(bk, 0, 128), g8, g8, True, True)])
+    cp(full("BO"), ref(bk, 0, 128))
+    act(full("BOn"), full("BO"), F.Copy, 0.0, -1.0)
+    cp(full("BOh"), full("BO"))
+    cp(full("Ib"), full("If"))
+    cp(full("Ih"), full("If"))
+    act(full("Inb"), full("If"), F.Copy, 0.0, -1.0)
+    act(full("Ihalf"), full("If"), F.Copy, 0.0, 0.5)
+    act(full("I16b"), full("If"), F.Copy, 0.0, 16.0)
+    ts(ref("PI", 16, 17), ref("PI", 0, 1), 15, A.bitwise_and)
+    ts(ref("PI", 24, 25), ref("PI", 0, 1), 1, A.bitwise_and)
+    pm, sg = ref("PC", 0, 1), ref("PC", 4, 5)
+    cp(pm, ref("PI", 16, 17))
+    ts(sg, ref("PI", 24, 25), -2.0, A.mult, 1.0, A.add)
+    cp(ref("WTf", 0, 2), full("WT"))
+    wcol, kcol = ref("WTf", 0, 1), ref("WTf", 1, 2)
+    act(full("WB"), full("BO"), F.Copy, 0.0, wcol)
+    fill(full("Bh"), 0.0)
+    cp(ref("Bh", 15, 143, 16), ref("BO", 0, 128, 16))
+    fill(full("CLB"), 8192.0)
+    CL = ref("CLB", 0, 1)
+    ts(full("B32"), ref("BO", 0, 128, 16), 32.0, A.mult)
+    ts(full("Bm16"), ref("BO", 0, 128, 16), -16.0, A.mult)
+    ts(full("OJ"), full("IJ"), pm, A.is_equal, 613.0, A.mult)
+    ts(full("OK"), full("IJ"), pm, A.is_equal)
+    for j in range(16):
+        ts(ref("SJ", 128 * j, 128 * j + 128), full("BOh"), ref("OJ", j, j + 1), A.mult)
+    for j in range(16):
+        act(ref("SJb", 128 * j, 128 * j + 128), full("BO"), F.Copy, 0.0, ref("OK", j, j + 1))
+    ts(ref("CM", 0, 8), full("CMI"), pm, A.add)
+    ts(ref("CM", 8, 16), ref("CM", 0, 8), float(2 * n), A.add)
+    ts(ref("CM", 16, 24), ref("CM", 0, 8), float(3 * n), A.add)
+    for h in range(2):
+        ts(sm("CMm", h), ref("CM", 0, 8), float(n * h), A.add)
+    consts = (-9.0, 8192.0, -4096.0, 2048.0, -100.0, 1.0, 100.0)
+    for i, c in enumerate(consts):
+        fill(ref("CON", 8 * i, 8 * i + 8), c)
+    con = lambda c: ref("CON", 8 * consts.index(c), 8 * consts.index(c) + 8)
+    for nm, src, c in (("In", "Ih", float(n)), ("I2n", "Ih", float(2 * n)), ("Ip100", "Ih", 100.0), ("Im100", "Ih", -100.0), ("I8", "Ih", 8.0),
+                       ("I8k", "Ih", 8192.0), ("I8kn", "Ih", -8192.0), ("BO613", "BOh", 613.0), ("I8184", "Ih", -8184.0)):
+        ts(full(nm), full(src), c, A.mult)
+    ts(full("G0"), full("Ih"), sg, A.mult)
+    tt(full("Gn"), full("G0"), full("In"), A.add)
+    tt(full("G2n"), full("G0"), full("I2n"), A.add)
+    act(ref("Sb", 0, 128, 2), ref("If", 1, 128, 2), F.Copy)
+    act(ref("Sb", 1, 128, 2), ref("If", 0, 128, 2), F.Copy)
+    cp(full("Sh"), full("Sb"))
+    ts(full("Sh100"), full("Sb"), 100.0, A.mult)
+    fill(full("ON"), 1.0)
+    fill(full("CQ"), -0.25 / 128)
+    fill(full("MK"), 1.0)
+    fill(ref("MK", 0, 16 * n, 16), 0.0)
+    fill(full("MF"), 1.0)
+    fill(ref("MF", 0, n, 16), 0.0)
+    fill(full("RST"), 0.0)
+    fill(ref("RST", 0, 128, 16), 1048576.0)
+    fill(full("QS"), 0.0)
+    fill(full("C256"), 256.0)
+    fill(full("VS"), 0.0)
+    for k in range(8):
+        fill(ref("ZB", k * (32 + n) + 24, k * (32 + n) + 32), 0.0)
+
+    def ots(out, tile, base="Bh", first=(), last=()):
+        prs = list(first)
+        for j in range(16):
+            prs.append((ref(base, 15 - j, 143 - j), ref(tile[0], tile[1] + j, tile[2], 16)))
+        return acc(out, *(prs + list(last)))
+
+    def spread(out, src):
+        return [(ref(out[0], out[1] + j, out[2], 16), ref("SJ", 128 * j, 128 * j + 128), src, True, True) for j in range(16)]
+
+    ts(ref("VZi", 0, 256), ref("VZ", 0, 256), 4032, A.bitwise_and)
+    cp(ref("VZh", 0, 256), ref("VZi", 0, 256))
+    ts(ref("VZi", 256, 512), ref("VZ", 0, 256), 63, A.bitwise_and)
+    cp(ref("VZh", 256, 512), ref("VZi", 256, 512))
+    cp(ref("VZh", 512, 768), ref("VZ", 256, 512))
+
+    def s16(c0):
+        return [(ref("Bh", 15 - j, 143 - j), ref("VZh", c0 + j, c0 + 256, 16)) for j in range(16)]
+    pe(acc(ref("b6", 0, 16), *(s16(0) + s16(256))))
+    pe(acc(ref("b5", 0, 16), *s16(512)))
+    for h in (1, 0):
+        ts(ref("VH", 8 * h, 8 * h + 8), ref("b6", 8 * h, 8 * h + 8), -2048.0, A.add)
+        fill(ref("XZ", h * XW, h * XW + 16), 0.0)
+        ts(ref("XZ", h * XW + 16, h * XW + 24), ref("b5", 8 * h, 8 * h + 8), 1.0, A.add)
+        cp(ref("W", h * WW + n, h * WW + 2 * n), ref("FI", h * n, h * n + n))
+    for c in range(2):
+        x = ref("VW", 1024 * c, 1024 * c + 1024)
+        it = full("IT")
+        ts(it, x, 4095, A.bitwise_and)
+        cp(ref("VI", 1024 * c, 1024 * c + 1024), it)
+        ts(x, x, 12, A.arith_shift_right)
+        cp(ref("VI", 2048 + 1024 * c, 3072 + 1024 * c), x)
+
+    def tiles(t, h):
+        k = 2 * t + h
+        x0, w0 = k * XW, k * WW
+        return {"cnt": lambda j: ref("XZ", x0 + 8 * j, x0 + 8 * j + 8), "z": ref("XZ", x0 + 32, x0 + 32 + n), "x": ref("XZ", x0 + 32 + n, x0 + 32 + 2 * n),
+                "hz": ref("XZ", x0 + 32 + 2 * n, x0 + 32 + 3 * n), "xz": ref("XZ", x0 + 32, x0 + 32 + 2 * n), "xzh": ref("XZ", x0 + 32, x0 + 32 + 3 * n),
+                "hd": ref("W", w0, w0 + n), "f": ref("W", w0 + n, w0 + 2 * n), "e": ref("W", w0 + 2 * n, w0 + 3 * n), "c": ref("W", w0 + 3 * n, w0 + 4 * n),
+                "w2": ref("W", w0, w0 + 2 * n), "w3": ref("W", w0, w0 + 3 * n), "w4": ref("W", w0, w0 + 4 * n), "vh": ref("VH", 8 * k, 8 * k + 8),
+                "land": ref("XZ", x0, x0 + 32 + n), "zb": ref("ZB", k * (32 + n), (k + 1) * (32 + n)), "zf": ref("ZB", k * (32 + n) + 32, (k + 1) * (32 + n)),
+                "zc": ref("ZB", k * (32 + n), k * (32 + n) + 24), "fb": ref("FB", k * n, k * n + n), "vb": ref("VB", 8 * k, 8 * k + 8)}
+
+    px, views = full("PX"), ref("VI", 0, 4096)
+    vks = {}
+
+    def front(t, h):
+        pg["st"] = BIAS * h
+        L = tiles(t, h)
+        otl = sm("OTL", h)
+        ts(otl, L["vh"], 2048.0, A.add)
+        act(L["x"], ("ind", px, otl), F.Copy)
+        act(L["e"], ("ind", views, otl), F.Copy)
+        bk = bank(h)
+        vk = ref(bank(h), 0, n)
+        vks[h] = vk
+        dx = ref(bk, 0, n)
+        pe(acc(dx, (full("Ib"), L["x"]), (full("Inb"), L["z"])))
+        y = ref(bank(h), 0, n)
+        pe(acc(y, (full("WB"), L["z"])))
+        act(tl("AB", h), dx, F.Abs)
+        ts(tl("IND", h), tl("AB", h), 72.0, A.is_le)
+        pe([(vk, full("BO613"), full("C256"), True, False)]
+           + [(ref(vk[0], j, n, 16), ref("SJ", 128 * j, 128 * j + 128), L["vh"], False, j == 15) for j in range(16)])
+        ct = ref(bank(h), 0, 8)
+        pe(ots(ct, tl("IND", h), "Bh", [(full("Ih"), con(-9.0))], [(full("Inb"), L["cnt"](1))]))
+        lk = sm("LK", h)
+        ts(lk, ct, -0.5, A.is_ge)
+        b = bank(h)
+        pe(acc(ref(b, 0, 8), (full("Ih"), ref("CM", 0, 8)), (full("In"), lk)) + acc(ref(b, 8, 16), (full("Ih"), ref("CM", 0, 8)), (full("I2n"), lk))
+           + acc(ref(b, 16, 24), (full("Ih"), L["vh"]), (full("Ih"), con(-4096.0)), (full("I8k"), lk)))
+        cp(sm("LSL", h, 16, 0, 16), ref(b, 0, 16))
+        act(ref("VS", h * n, h * n + n, 16), ref(b, 16, 24), F.Relu, 0.0, 613.0)
+        q0 = h * 16 * n
+        ts(ref("QS", 0, 16 * n, 16), ("ind", L["xz"], sm("LSL", h, 16)), -512.0, A.add)
+        scan(ref("QX", q0, q0 + 16 * n), full("MK"), full("QS"), 0.0, A.mult, A.add)
+        a, c = tl("HI1", h), tl("HI2", h)
+        cp(a, y)
+        ts(c, a, 4095, A.bitwise_and)
+        ts(a, c, kcol, A.mult, -65536.0, A.add)
+        ts(c, a, 5, A.arith_shift_right)
+        tt(a, c, vk, A.add)
+        ts(c, a, 4095, A.bitwise_and)
+        cp(L["hd"], c)
+        scan(tl("VR", h), full("MF"), tl("VS", h), 0.0, A.mult, A.add)
+        tt(tl("EQ", h), tl("VR", h), vk, A.is_equal)
+        for i in range(2):
+            he = ref("HE", (2 * h + i) * n, (2 * h + i + 1) * n)
+            act(he, ("ind", L["w2"] if i == 0 else L["w3"], sm("LSL", h, 16, 8 * i)), F.Copy)
+            cp(ref("HEL", (2 * h + i) * n, (2 * h + i + 1) * n), he)
+
+    def dedupe(t, h):
+        pg["st"] = BIAS * h
+        L = tiles(t, h)
+        lk = sm("LK", h)
+        du = ref(bank(h), 0, 8)
+        pe(acc(du, *([(ref("LTJ", 128 * j, 128 * j + 128), ref("EQ", h * n + j, h * n + n, 16)) for j in range(16)] + [(full("Ih"), con(100.0)), (full("Im100"), lk)])))
+        ts(sm("W0", h), du, 0.5, A.is_lt)
+        vd = ref(bank(h), 0, 8)
+        pe(acc(vd, (full("Ih"), con(2048.0)), (full("Ih"), sm("CMm", h)), (full("I8kn"), sm("W0", h))))
+        tt(sm("O2", h), L["vh"], vd, A.max)
+        ts(ref("OFF", h * 16, h * 16 + 16, 2), sm("O2", h), 2048.0, A.add)
+
+    def early(t, h):
+        pg["st"] = BIAS * h
+        L = tiles(t, h)
+        lk, d1, ov = sm("LK", h), sm("D1", h), sm("OV", h)
+        Ih, Ib, Sh, Sb, Ip, Im = full("Ih"), full("Ib"), full("Sh"), full("Sb"), full("Ip100"), full("Im100")
+        hz = ref(bank(h), 0, n)
+        pe(acc(hz, (full("Ihalf"), L["x"]), (full("Ihalf"), L["z"]), (full("CQ"), full("ON"))))
+        act(tl("T1", h), hz, F.Identity, MAGIC)
+        act(L["hz"], tl("T1", h), F.Identity, -MAGIC)
+        dp = ref(bank(h), 0, 8)
+        pe(acc(dp, (Ib, L["cnt"](2)), (Im, lk)))
+        act(d1, dp, F.Relu)
+        po = ref(bank(h), 0, 8)
+        pe(acc(po, (Ib, d1), (full("Sh100"), lk)))
+        ts(ov, po, 101.5, A.is_ge)
+        b = bank(h)
+        pe(acc(ref(b, 0, 8), (Ih, ref("CM", 0, 8)), (full("I2n"), lk), (full("G2n"), ov))
+           + acc(ref(b, 8, 16), (Ih, ref("CM", 8, 16)), (full("In"), lk), (full("Gn"), ov))
+           + acc(ref(b, 16, 24), (Ih, ref("CM", 16, 24)), (full("G0"), ov)))
+        cp(sm("TLL", h, 24, 0, 24), ref(b, 0, 24))
+        act(L["zf"], ("ind", L["xzh"], sm("TLL", h, 24)), F.Copy)
+        pp = ref(bank(h), 0, 8)
+        pe(acc(pp, (Ih, lk), (full("Inb"), L["cnt"](1))))
+        act(sm("P1", h), pp, F.Abs)
+        b = bank(h)
+        p1, ca = sm("P1", h), L["cnt"](0)
+        pe(acc(ref(b, 0, 8), (Ib, ca), (Ih, lk), (Im, ov)) + acc(ref(b, 8, 16), (Sb, ca), (Sh, lk), (Ip, ov), (Ih, con(-100.0)))
+           + acc(ref(b, 16, 24), (Ib, p1), (Im, ov)) + acc(ref(b, 24, 32), (Sb, p1), (Ip, ov), (Ih, con(-100.0))) + acc(ref(b, 32, 40), (Ib, d1), (Im, ov)))
+        ra = lambda j: sm("RA", h, 40, 8 * j)
+        act(sm("RA", h, 40, 0, 40), ref(b, 0, 40), F.Relu)
+        b = bank(h)
+        if t < NT - 1:
+            pe(acc(ref(b, 0, 8), (Ib, ra(0)), (Ib, ra(1))) + acc(ref(b, 8, 16), (Ib, ra(2)), (Ib, ra(3))) + acc(ref(b, 16, 24), (Ib, ra(4)), (Ih, con(1.0))))
+            act(L["zc"], ref(b, 0, 24), F.Copy)
+            send("z", t + 1, h, tiles(t + 1, h)["land"], L["zb"])
+        else:
+            i16 = full("I16b")
+            pe(acc(ref(b, 0, 8), (i16, ra(0)), (i16, ra(1)), (Ib, ra(4))))
+            cp(sm("YC", h), ref(b, 0, 8))
+            b = ref(bank(h), 0, n)
+            pe(spread(b, sm("YC", h)))
+            ts(tl("YI", h), b, 1.0 / 613.0, A.mult)
+            cp(ref("YU", h * n, h * n + n), tl("YI", h))
+            store(T.yc[:, h * n:h * n + n], ref("YU", h * n, h * n + n, 1, 0, 128, 16))
+            cp(ref("YU", 1024 + h * n, 1024 + h * n + n), L["zf"])
+            store(T.yz[:, h * n:h * n + n], ref("YU", 1024 + h * n, 1024 + h * n + n))
+        cb = ref(bank(h), 0, 8)
+        pe(acc(cb, (Ih, con(8192.0)), (full("I8kn"), lk), (full("I8184"), ov)))
+        act(sm("CB", h), cb, F.Copy)
+        y = ref(bank(h), 0, n)
+        pe([(y, full("BO"), L["zf"], True, False)]
+           + [(ref(y[0], j, n, 16), ref("SJb", 128 * j, 128 * j + 128), sm("CB", h), False, j == 15) for j in range(16)])
+        ts(tl("KI", h), y, float(t), A.add)
+        ts(tl("KJ", h), tl("KI", h), 8192 + 15, A.bitwise_and)
+        ts(tl("OHL", h), tl("KJ", h), pm, A.is_equal)
+        act(tl("RL", h), y, F.Relu, CL, -1.0)
+
+    def bulk(t, h):
+        pg["st"] = BIAS * h
+        L = tiles(t, h)
+        q0, e0 = h * 16 * n, h * 2 * n
+        key = tl("KEY", h)
+        bh_, be_ = bank(h), bank(h)
+
+        def part(G, D, R, l0, a, b, fused):
+            g_, d_, r_ = ref(G, q0 + 16 * a, q0 + 16 * b), ref(D, q0 + 16 * a, q0 + 16 * b), ref(R, q0 + 16 * a, q0 + 16 * b)
+            off = ref("HEL", l0 + a, l0 + b)
+            qx = ref("QX", q0 + 16 * a, q0 + 16 * b)
+            if fused:
+                tt(d_, ("ind", px, off), qx, A.subtract)
+            else:
+                act(g_, ("ind", px, off), F.Copy)
+                scan(d_, g_, qx, 600.0, A.min, A.subtract)
+            ts(r_, d_, 512.0, A.max)
+
+        def sums(out, D, R, first):
+            mm = []
+            if first:
+                mm.append((out, full("Ib"), full("KC"), True, False))
+            for k in range(16):
+                o = ref(out[0], out[1] + k, out[2], 16)
+                mm.append((o, ref(R, q0 + k, q0 + 16 * n, 16), full("B32"), not first, False))
+                mm.append((o, ref(D, q0 + k, q0 + 16 * n, 16), full("Bm16"), False, (not first) or k == 15))
+            pe(mm)
+        ph, pd = ref(bh_, 0, n), ref(be_, 0, n)
+        part("GH", "DH", "RH", e0, 0, n // 2, False)
+        part("GH", "DH", "RH", e0, n // 2, n, False)
+        sums(ph, "DH", "RH", True)
+        act(key, ph, F.Copy)
+        he1, he2 = ref("HE", e0, e0 + n), ref("HE", e0 + n, e0 + 2 * n)
+        tt(tl("HME", h), he1, he2, A.subtract)
+        scan(tl("PM", h), full("RST"), key, 0.0, A.add, A.min)
+        mn = ref(bank(h), 0, n, 1, 0, 8)
+        pe([(mn, ref("PM", h * n + 15, h * n + n, 16), full("If"), True, True)])
+        mns = ref("MN", h * n, h * n + n, 1, 0, 8)
+        act(mns, mn, F.Copy)
+        mx = ref(bank(h), 0, n)
+        pe([(mx, mns, g8, True, False), (mx, tl("RL", h), full("BOn"), False, True)])
+        tt(tl("OHT", h), key, mx, A.is_equal)
+        if NE > 0:
+            part("GE", "DE", "RE", e0 + n, 0, NE, False)
+        if NE < n:
+            part("GE", "DE", "RE", e0 + n, NE, n, True)
+        sums(pd, "DE", "RE", False)
+        tt(tl("MT", h), key, pd, A.is_lt)
+        mk = ref(bank(h), 0, n)
+        pe([(mk, tl("MT", h), full("Ib"), True, True)])
+        tt(tl("MM", h), tl("HME", h), mk, A.mult)
+        tt(L["c"], tl("MM", h), he2, A.add)
+        act(tl("CF", h), ("ind", L["w4"], sm("TLL", h, 24, 16)), F.Identity, -2048.0)
+        oc = ref(bank(h), 0, n)
+        pe([(oc, tl("OHT", h), full("Ib"), True, False), (oc, full("Ib"), tl("OHL", h), False, True)])
+        tt(tl("PP", h), tl("CF", h), oc, A.mult)
+        vo = ref(bank(h), 0, n)
+        if t < NT - 1:
+            vo = ref(vo[0], 0, 8)
+            pe(ots(vo, tl("PP", h)))
+            cp(L["vb"], vo)
+            send("v", t + 1, h, tiles(t + 1, h)["vh"], L["vb"])
+        else:
+            pe(acc(vo, (full("BOh"), tl("PP", h))))
+            ts(ref("YU", 512 + h * n, 512 + h * n + n), vo, 2048.0, A.add)
+            store(T.yv[:, h * n:h * n + n], ref("YU", 512 + h * n, 512 + h * n + n, 1, 0, 128, 16))
+        act(L["fb"], ("ind", L["w4"], sm("TLL", h, 24, 8)), F.Copy)
+        if t < NT - 1:
+            send("f", t + 1, h, tiles(t + 1, h)["f"], L["fb"])
+        else:
+            store(T.yf[:, h * n:h * n + n], L["fb"])
+
+    def scatter(t, h):
+        pg["st"] = BIAS * h
+        L = tiles(t, h)
+        c0 = L["c"][1]
+        for c in range(7, -1, -1):
+            add(pg, "V", 0.12, lambda e, c=c: e.tensor_copy(ap(full("VI")).indirect(ap(ref("OFF", h * 16 + 2 * c, h * 16 + 2 * c + 1))), ap(ref("W", c0 + 16 * c, c0 + 16 * c + 16))),
+                [ref("OFF", h * 16 + 2 * c, h * 16 + 2 * c + 1), ref("W", c0 + 16 * c, c0 + 16 * c + 16)], [full("VI")], tag="scatter")
+
+    front(0, 1)
+    sel(full("BOg"), full("BO"), [[1, 128]], A.is_gt, 0.0, 0, -1)
+    iota(full("LTJ"), [[0, 2048]], 0, 0, True)
+    for j in range(16):
+        act(ref("LTJ", 128 * j + j, 128 * j + 128, 16), ref("BOg", j, 128, 16), F.Copy)
+    fill(ref("VI", 4096, 4096 + 2 * n), 0.0)
+    front(0, 0)
+    for t in range(NT):
+        for h in (1, 0):
+            if t > 0 and h == 1:
+                pass
+            early(t, h)
+            dedupe(t, h)
+            bulk(t, h)
+            scatter(t, h)
+            if t < NT - 1 and h == 1:
+                pass
+        if t < NT - 1:
+            front(t + 1, 1)
+            front(t + 1, 0)
+    for c in range(4):
+        a, b = 512 * c, 512 * c + 512
+        act(ref("YT", a, b), ref("VI", 2048 + a, 2048 + b), F.Copy, 0.0, 4096.0)
+        tt(ref("YT", a, b), ref("YT", a, b), ref("VI", a, b), A.add)
+        store(T.yw[:, a:b], ref("YT", a, b))
+    pg["nls"], pg["nout"] = nls[0], nout[0]
+    return pg
+
+
+def rank_program(g, core, T, topo):
+    rank = T.rank_of(core)
+    if rank is None:
+        return
+    pg = build(T, topo, core, rank)
+    schedule(pg)
+    emit(pg, g, T)
+    g.wait_ge(T.sem["ls"], int(pg["nls"]))
+    g.wait_ge(T.sem["out"], int(pg["nout"]))

@@ -9,8 +9,9 @@ NT = 5
 XW = 32 + 3 * n
 WW = 4 * n
 MAGIC = 12582912.0
-BIAS = 10.0
-NE = 64
+PRI = {'fr0': 5.1, 'fr1': 10.5, 'qx0': -9.6, 'qx1': -8.0, 'ha0': 12.2, 'ha1': -1.7, 'dd0': -0.6, 'dd1': 5.7, 'h0': -4.5, 'h1': -5.5, 'e0': -9.4, 'e1': 0.6, 'ea0': -3.8, 'ea1': 1.7, 'kk0': -0.1,
+       'kk1': 11.4, 'hb0': -6.6, 'hb1': -5.1, 'hm0': 4.1, 'hm1': -8.8, 'km0': -5.6, 'km1': -2.7, 'eb0': 4.0, 'eb1': -3.3, 'cc0': -4.9, 'cc1': 12.0, 'ff0': 1.5, 'ff1': 16.4, 'sc0': -17.9, 'sc1': -15.7}
+NE = 80
 f4, b2, h2, i4, u2 = "float32", "bfloat16", "float16", "int32", "uint16"
 
 SCRATCH = {
@@ -24,7 +25,8 @@ SCRATCH = {
     "OTL": ("sbuf", [128, 16], u2), "AB": ("sbuf", [128, 2 * n], b2), "IND": ("sbuf", [128, 2 * n], h2), "LK": ("sbuf", [128, 16], h2),
     "LSL": ("sbuf", [128, 32], u2), "HI1": ("sbuf", [128, 2 * n], i4), "HI2": ("sbuf", [128, 2 * n], i4), "T1": ("sbuf", [128, 2 * n], f4),
     "D1": ("sbuf", [128, 16], b2), "OV": ("sbuf", [128, 16], h2), "TLL": ("sbuf", [128, 48], u2), "P1": ("sbuf", [128, 16], b2), "RA": ("sbuf", [128, 80], b2),
-    "KI": ("sbuf", [128, 2 * n], i4), "KJ": ("sbuf", [128, 2 * n], i4), "CB": ("sbuf", [128, 16], b2), "SJb": ("sbuf", [128, 2048], b2), "OK": ("sbuf", [128, 16], f4), "CLB": ("sbuf", [128, 8], f4), "OHL": ("sbuf", [128, 2 * n], b2), "RL": ("sbuf", [128, 2 * n], b2),
+    "KI": ("sbuf", [128, 2 * n], i4), "KJ": ("sbuf", [128, 2 * n], i4), "CB": ("sbuf", [128, 16], b2), "SJb": ("sbuf", [128, 2048], b2), "OK": ("sbuf", [128, 16], f4), "CLB": ("sbuf", [128, 8], f4),
+    "WBs": ("sbuf", [128, 128], b2), "I4kn": ("sbuf", [128, 128], b2), "CH": ("sbuf", [128, 128], b2), "T2": ("sbuf", [128, 2 * n], f4), "FL": ("sbuf", [128, 2 * n], b2), "EQ2": ("sbuf", [128, 2 * n], h2), "OHL": ("sbuf", [128, 2 * n], b2), "RL": ("sbuf", [128, 2 * n], b2),
     "VS": ("sbuf", [128, 2 * n], f4), "VR": ("sbuf", [128, 2 * n], f4), "EQ": ("sbuf", [128, 2 * n], b2),
     "W0": ("sbuf", [128, 16], h2), "O2": ("sbuf", [128, 16], f4), "OFF": ("sbuf", [128, 32], u2),
     "HME": ("sbuf", [128, 2 * n], f4), "KEY": ("sbuf", [128, 2 * n], f4), "MT": ("sbuf", [128, 2 * n], b2), "MM": ("sbuf", [128, 2 * n], f4),
@@ -38,9 +40,9 @@ SCRATCH = {
     "Bh": ("sbuf", [128, 144], h2), "B32": ("sbuf", [128, 8], h2), "Bm16": ("sbuf", [128, 8], h2),
     "SJ": ("sbuf", [128, 2048], h2), "LTJ": ("sbuf", [128, 2048], b2), "PI": ("sbuf", [128, 32], i4), "PC": ("sbuf", [128, 16], f4),
     "OJ": ("sbuf", [128, 16], f4),  "IJ": ("sbuf", [128, 16], f4), "CMI": ("sbuf", [128, 8], f4), "CM": ("sbuf", [128, 24], h2), "CMm": ("sbuf", [128, 16], h2),
-    "CON": ("sbuf", [128, 64], h2), "KC": ("sbuf", [128, 128], b2), "MK": ("sbuf", [128, 16 * n], h2), "MF": ("sbuf", [128, n], f4), "RST": ("sbuf", [128, 128], f4),
+    "CON": ("sbuf", [128, 64], h2), "KC": ("sbuf", [128, 128], b2), "MK": ("sbuf", [128, 16 * n], b2), "MF": ("sbuf", [128, n], f4), "RST": ("sbuf", [128, 128], f4),
     "CQ": ("sbuf", [128, 128], b2), "ON": ("sbuf", [128, 128], b2), "WT": ("sbuf", [128, 2], i4), "WTf": ("sbuf", [128, 8], f4),
-    "VZ": ("sbuf", [128, 512], i4), "VZi": ("sbuf", [128, 512], i4), "VZh": ("sbuf", [128, 768], h2), "FI": ("sbuf", [128, 256], i4), "YC": ("sbuf", [128, 16], h2), "YI": ("sbuf", [128, 2 * n], i4),
+    "VZ": ("sbuf", [128, 512], i4), "VZi": ("sbuf", [128, 512], i4), "VZh": ("sbuf", [128, 768], h2), "FI": ("sbuf", [128, 256], i4), "YC": ("sbuf", [128, 16], b2),
 }
 for _b in range(8):
     SCRATCH["b%d" % _b] = ("psum", [128, 512], f4)
@@ -53,7 +55,7 @@ def ref(name, c0, c1, step=1, p0=0, p1=128, pstep=1):
 
 
 def new_prog():
-    return {"ops": [], "acc": {}, "rr": [0, 0], "st": 0.0}
+    return {"ops": [], "acc": {}, "rr": [0], "st": "", "bmap": {}}
 
 
 def touch(pg, o, r, wr):
@@ -69,8 +71,8 @@ def touch(pg, o, r, wr):
             if psum:
                 if ops[p]["q"] != o["q"]:
                     o["dep"].add(p)
-                elif over and (wr or aw) and not (ops[p]["q"] == "P"):
-                    o["dep"].add(p)
+                elif o["q"] == "P":
+                    o["ord"].add(p)
             elif over and (wr or aw):
                 if aw or ops[p]["q"] != o["q"]:
                     o["dep"].add(p)
@@ -86,16 +88,22 @@ def touch(pg, o, r, wr):
 
 
 def add(pg, q, cost, fn, rd, wr, sem=None, val=1, after=(), lat=0.0, tag=""):
-    o = {"i": len(pg["ops"]), "q": q, "cost": cost, "fn": fn, "dep": set(after), "ord": set(), "sem": sem, "val": val, "lat": lat, "send": None, "tag": tag, "st": pg["st"]}
+    o = {"i": len(pg["ops"]), "q": q, "cost": cost, "fn": fn, "dep": set(after), "ord": set(), "sem": sem, "val": val, "lat": lat, "send": None, "tag": tag, "st": pg["st"], "wake": WAKE}
     pg["ops"].append(o)
     for r in rd:
         touch(pg, o, r, False)
     for r in wr:
         touch(pg, o, r, True)
+    o["tiles"] = sorted(set(r[0] for r in list(rd) + list(wr) if r[0][0] == "b" and r[0][1:].isdigit()))
+    o["dyn"] = set()
     return o["i"]
 
 
 WAKE = 0.10
+GC = 1.5
+PEC = 0.00055
+CY = 0.00083
+LNK = 1.6
 FIX = {"V": 0.03, "S": 0.04, "P": 0.03, "G": 0.05, "Y": 0.05}
 
 
@@ -116,7 +124,16 @@ def schedule(pg):
         i = o["i"]
         pri[i] = max([pri[s] for s in succ[i]] + [0.0]) + o["cost"] + o["lat"] + WAKE
     for o in ops:
-        pri[o["i"]] += o["st"]
+        pri[o["i"]] += PRI.get(o["st"], 0.0)
+    uses, first = {}, {}
+    for o in ops:
+        for tname in o["tiles"]:
+            if tname not in uses:
+                uses[tname] = 0
+                first.setdefault(o["i"], []).append(tname)
+            uses[tname] += 1
+    bfree = {b: (0.0, []) for b in range(8)}
+    bmap, held, late = {}, {}, {}
     ready = {}
     avail = [0.0] * N_
     free = {}
@@ -135,19 +152,48 @@ def schedule(pg):
                 cand = (avail[lst[0]], q, lst[0])
             else:
                 fr = free.get(q, 0.0)
-                st = min(max(fr, avail[i]) for i in lst)
-                c = [i for i in lst if max(fr, avail[i]) <= st + 0.02]
+                full_ = lst
+                if q == "P":
+                    if not bfree:
+                        lst = [i for i in lst if i not in first]
+                        if not lst:
+                            continue
+                    else:
+                        bt = min(v[0] for v in bfree.values())
+                        for i in lst:
+                            if i in first and avail[i] < bt:
+                                late[i] = bt
+                st = min(max(fr, avail[i], late.get(i, 0.0)) for i in lst)
+                c = [i for i in lst if max(fr, avail[i], late.get(i, 0.0)) <= st + 0.02]
                 cand = (st, q, max(c, key=lambda i: pri[i]))
             if best is None or cand[0] < best[0]:
                 best = cand
+        if best is None:
+            pg["fin"] = 1e6
+            return
         st, q, i = best
         ready[q].remove(i)
+        late.clear()
         o = ops[i]
+        o["dyn"] = set()
+        for tname in first.get(i, ()):
+            b = min(bfree, key=lambda b: bfree[b][0])
+            o["dyn"] |= set(bfree.pop(b)[1])
+            bmap[tname] = b
+            held[tname] = [0.0, []]
         end = st + o["cost"]
         free[q] = end
         fin[i] = end + o["lat"]
         order.setdefault(q, []).append(i)
         left -= 1
+        for tname in o["tiles"]:
+            hd = held[tname]
+            hd[0] = max(hd[0], end + WAKE)
+            if q != "P":
+                hd[1].append(i)
+            uses[tname] -= 1
+            if uses[tname] == 0:
+                bfree[bmap[tname]] = (hd[0], hd[1])
         for s in succ[i]:
             cnt[s] -= 1
             w = 0.0 if i in ops[s]["ord"] else WAKE
@@ -156,6 +202,8 @@ def schedule(pg):
                 ready.setdefault(ops[s]["q"], []).append(s)
         o["t0"], o["t1"] = st, end
     pg["order"] = order
+    pg["bmap"].clear()
+    pg["bmap"].update(bmap)
     pg["fin"] = max(fin)
     pg["seq"] = sorted(range(N_), key=lambda i: (ops[i]["t0"], ops[i]["q"][0] != "R", i))
 
@@ -185,6 +233,8 @@ def emit(pg, g, T):
             while state[q] < len(queues[q]):
                 i = queues[q][state[q]]
                 o = ops[i]
+                if o["dyn"]:
+                    o["dep"] |= o["dyn"]
                 if any(d not in done for d in o["dep"]) or (o["send"] is not None and o["send"] not in done):
                     break
                 kn = qk.setdefault(q, {})
@@ -231,12 +281,9 @@ def emit(pg, g, T):
 
 def build(T, topo, core, rank):
     pg = new_prog()
-    CY = 0.00083
-    GC = 1.5
-
     def ap(r):
         name, c0, c1, step, p0, p1, ps = r
-        t = T[name]
+        t = T["b%d" % pg["bmap"][name]] if name in pg["bmap"] else T[name]
         rows = slice(p0, p1) if ps == 1 else slice(p0, p1, ps)
         cols = slice(c0, c1) if step == 1 else slice(c0, c1, step)
         return t[rows, cols]
@@ -245,7 +292,7 @@ def build(T, topo, core, rank):
         return (r[2] - r[1] + r[3] - 1) // r[3]
 
     def two(*rs):
-        return all(SCRATCH[r[0]][2] in (b2, h2, u2) for r in rs)
+        return all(r[0] in SCRATCH and SCRATCH[r[0]][2] in (b2, h2, u2) for r in rs)
 
     def inap(x):
         if x[0] == "ind":
@@ -297,7 +344,7 @@ def build(T, topo, core, rank):
         rd, wr = {}, {}
         for out, l, r, s, e_ in mms:
             k = 4 if SCRATCH[l[0]][2] == f4 else 1
-            cost += 0.00055 * k * max(min(64, cnt(l)), cnt(r)) + 0.006
+            cost += PEC * k * max(min(64, cnt(l)), cnt(r)) + 0.006
             for x in (l, r):
                 y = rd.get(x[0])
                 rd[x[0]] = (x[0], min(x[1], y[1]) if y else x[1], max(x[2], y[2]) if y else x[2], 1, 0, 128, 1)
@@ -315,9 +362,8 @@ def build(T, topo, core, rank):
         return [(out, l, r, i == 0, i == len(pairs) - 1) for i, (l, r) in enumerate(pairs)]
 
     def bank(h, w=n):
-        b = 4 * h + pg["rr"][h] % 4
-        pg["rr"][h] += 1
-        return "b%d" % b
+        pg["rr"][0] += 1
+        return "b%d" % (99 + pg["rr"][0])
 
     def load(name, out, src, q="Y"):
         s = "ld_" + name
@@ -338,7 +384,7 @@ def build(T, topo, core, rank):
     def send(kind, t, h, out, in_):
         s = "r%s_%d_%d" % (kind, t, h)
         nls[0] += neng
-        i = add(pg, "G", 0.4, lambda e: e.remote_dma(ap(out), ap(in_), T.sem[s], T.sem["ls"], pid, rid, mask), [in_], [], sem="ls", val=nls[0], lat=1.6, tag="send " + s)
+        i = add(pg, "G", 0.4, lambda e: e.remote_dma(ap(out), ap(in_), T.sem[s], T.sem["ls"], pid, rid, mask), [in_], [], sem="ls", val=nls[0], lat=LNK, tag="send " + s)
         j = add(pg, "R" + s, 0.0, None, [], [out], sem=s, val=neng)
         pg["ops"][j]["send"] = i
 
@@ -378,7 +424,7 @@ def build(T, topo, core, rank):
     iota(full("CMI"), [[16, 8]], 0, 0, True)
     iota(full("KC"), [[0, 8], [1, 16]], 0, 0, True)
     g8 = ref("G8", 0, 128, 1, 0, 8)
-    bk = "b7"
+    bk = bank(0)
     pe([(ref(bk, 0, 128), g8, g8, True, True)])
     cp(full("BO"), ref(bk, 0, 128))
     act(full("BOn"), full("BO"), F.Copy, 0.0, -1.0)
@@ -398,8 +444,13 @@ def build(T, topo, core, rank):
     act(full("WB"), full("BO"), F.Copy, 0.0, wcol)
     fill(full("Bh"), 0.0)
     cp(ref("Bh", 15, 143, 16), ref("BO", 0, 128, 16))
-    fill(full("CLB"), 8192.0)
-    CL = ref("CLB", 0, 1)
+    fill(ref("CLB", 0, 4), 8192.0)
+    fill(ref("CLB", 4, 8), -65536.0)
+    CL, HB = ref("CLB", 0, 1), ref("CLB", 4, 5)
+    act(full("WBs"), full("WB"), F.Copy, 0.0, 1.0 / 4096)
+    act(full("I4kn"), full("If"), F.Copy, 0.0, -4096.0)
+    fill(ref("CH", 0, 128, 1, 0, 64), -0.5 / 64)
+    fill(ref("CH", 0, 128, 1, 64, 128), 2.0 ** -19)
     ts(full("B32"), ref("BO", 0, 128, 16), 32.0, A.mult)
     ts(full("Bm16"), ref("BO", 0, 128, 16), -16.0, A.mult)
     ts(full("OJ"), full("IJ"), pm, A.is_equal, 613.0, A.mult)
@@ -429,8 +480,8 @@ def build(T, topo, core, rank):
     ts(full("Sh100"), full("Sb"), 100.0, A.mult)
     fill(full("ON"), 1.0)
     fill(full("CQ"), -0.25 / 128)
-    fill(full("MK"), 1.0)
-    fill(ref("MK", 0, 16 * n, 16), 0.0)
+    iota(full("MK"), [[0, 16 * n]], 1, 0, True)
+    sel(full("MK"), full("MK"), [[0, n], [1, 16]], A.not_equal, 0.0, 0, 0)
     fill(full("MF"), 1.0)
     fill(ref("MF", 0, n, 16), 0.0)
     fill(full("RST"), 0.0)
@@ -458,12 +509,13 @@ def build(T, topo, core, rank):
 
     def s16(c0):
         return [(ref("Bh", 15 - j, 143 - j), ref("VZh", c0 + j, c0 + 256, 16)) for j in range(16)]
-    pe(acc(ref("b6", 0, 16), *(s16(0) + s16(256))))
-    pe(acc(ref("b5", 0, 16), *s16(512)))
+    b6, b5 = bank(0), bank(0)
+    pe(acc(ref(b6, 0, 16), *(s16(0) + s16(256))))
+    pe(acc(ref(b5, 0, 16), *s16(512)))
     for h in (1, 0):
-        ts(ref("VH", 8 * h, 8 * h + 8), ref("b6", 8 * h, 8 * h + 8), -2048.0, A.add)
+        ts(ref("VH", 8 * h, 8 * h + 8), ref(b6, 8 * h, 8 * h + 8), -2048.0, A.add)
         fill(ref("XZ", h * XW, h * XW + 16), 0.0)
-        ts(ref("XZ", h * XW + 16, h * XW + 24), ref("b5", 8 * h, 8 * h + 8), 1.0, A.add)
+        ts(ref("XZ", h * XW + 16, h * XW + 24), ref(b5, 8 * h, 8 * h + 8), 1.0, A.add)
         cp(ref("W", h * WW + n, h * WW + 2 * n), ref("FI", h * n, h * n + n))
     for c in range(2):
         x = ref("VW", 1024 * c, 1024 * c + 1024)
@@ -486,8 +538,11 @@ def build(T, topo, core, rank):
     px, views = full("PX"), ref("VI", 0, 4096)
     vks = {}
 
+    def mark(name, h):
+        pg["st"] = name + str(h)
+
     def front(t, h):
-        pg["st"] = BIAS * h
+        mark("fr", h)
         L = tiles(t, h)
         otl = sm("OTL", h)
         ts(otl, L["vh"], 2048.0, A.add)
@@ -499,7 +554,7 @@ def build(T, topo, core, rank):
         dx = ref(bk, 0, n)
         pe(acc(dx, (full("Ib"), L["x"]), (full("Inb"), L["z"])))
         y = ref(bank(h), 0, n)
-        pe(acc(y, (full("WB"), L["z"])))
+        pe(acc(y, (full("WBs"), L["z"]), (full("CH"), full("ON"))))
         act(tl("AB", h), dx, F.Abs)
         ts(tl("IND", h), tl("AB", h), 72.0, A.is_le)
         pe([(vk, full("BO613"), full("C256"), True, False)]
@@ -514,37 +569,47 @@ def build(T, topo, core, rank):
         cp(sm("LSL", h, 16, 0, 16), ref(b, 0, 16))
         act(ref("VS", h * n, h * n + n, 16), ref(b, 16, 24), F.Relu, 0.0, 613.0)
         q0 = h * 16 * n
+        mark("qx", h)
         ts(ref("QS", 0, 16 * n, 16), ("ind", L["xz"], sm("LSL", h, 16)), -512.0, A.add)
         scan(ref("QX", q0, q0 + 16 * n), full("MK"), full("QS"), 0.0, A.mult, A.add)
         a, c = tl("HI1", h), tl("HI2", h)
-        cp(a, y)
-        ts(c, a, 4095, A.bitwise_and)
-        ts(a, c, kcol, A.mult, -65536.0, A.add)
+        mark("ha", h)
+        act(tl("T2", h), y, F.Identity, MAGIC)
+        act(tl("FL", h), tl("T2", h), F.Identity, -MAGIC)
+        um = ref(y[0], n, 2 * n)
+        pe(acc(um, (full("WB"), L["z"]), (full("I4kn"), tl("FL", h))))
+        act(tl("T2", h), um, F.Identity, HB, kcol)
+        cp(a, tl("T2", h))
         ts(c, a, 5, A.arith_shift_right)
         tt(a, c, vk, A.add)
         ts(c, a, 4095, A.bitwise_and)
         cp(L["hd"], c)
+        mark("dd", h)
         scan(tl("VR", h), full("MF"), tl("VS", h), 0.0, A.mult, A.add)
         tt(tl("EQ", h), tl("VR", h), vk, A.is_equal)
+        tt(ref("EQ2", h * n + 16, h * n + n), ref("VR", h * n, h * n + n - 16), ref(vk[0], 16, n), A.is_equal)
         for i in range(2):
+            mark("he"[i], h)
             he = ref("HE", (2 * h + i) * n, (2 * h + i + 1) * n)
             act(he, ("ind", L["w2"] if i == 0 else L["w3"], sm("LSL", h, 16, 8 * i)), F.Copy)
             cp(ref("HEL", (2 * h + i) * n, (2 * h + i + 1) * n), he)
 
     def dedupe(t, h):
-        pg["st"] = BIAS * h
+        mark("dd", h)
         L = tiles(t, h)
         lk = sm("LK", h)
         du = ref(bank(h), 0, 8)
-        pe(acc(du, *([(ref("LTJ", 128 * j, 128 * j + 128), ref("EQ", h * n + j, h * n + n, 16)) for j in range(16)] + [(full("Ih"), con(100.0)), (full("Im100"), lk)])))
+        m3 = acc(du, *([(full("Ih"), con(100.0)), (full("Im100"), lk)] + [(ref("LTJ", 128 * j, 128 * j + 128), ref("EQ", h * n + j, h * n + n, 16)) for j in range(16)]))
+        m3[-1] = m3[-1][:4] + (False,)
+        pe(m3 + [(ref(du[0], 1, 8, 2), ref("Bh", 15 - j, 143 - j), ref("EQ2", h * n + 16 + j, h * n + n, 32), False, j == 15) for j in range(16)])
         ts(sm("W0", h), du, 0.5, A.is_lt)
         vd = ref(bank(h), 0, 8)
         pe(acc(vd, (full("Ih"), con(2048.0)), (full("Ih"), sm("CMm", h)), (full("I8kn"), sm("W0", h))))
         tt(sm("O2", h), L["vh"], vd, A.max)
-        ts(ref("OFF", h * 16, h * 16 + 16, 2), sm("O2", h), 2048.0, A.add)
+        ts(sm("OFF", h), sm("O2", h), 2048.0, A.add)
 
     def early(t, h):
-        pg["st"] = BIAS * h
+        mark("ea", h)
         L = tiles(t, h)
         lk, d1, ov = sm("LK", h), sm("D1", h), sm("OV", h)
         Ih, Ib, Sh, Sb, Ip, Im = full("Ih"), full("Ib"), full("Sh"), full("Sb"), full("Ip100"), full("Im100")
@@ -581,14 +646,14 @@ def build(T, topo, core, rank):
         else:
             i16 = full("I16b")
             pe(acc(ref(b, 0, 8), (i16, ra(0)), (i16, ra(1)), (Ib, ra(4))))
-            cp(sm("YC", h), ref(b, 0, 8))
+            act(sm("YC", h), ref(b, 0, 8), F.Copy)
             b = ref(bank(h), 0, n)
-            pe(spread(b, sm("YC", h)))
-            ts(tl("YI", h), b, 1.0 / 613.0, A.mult)
-            cp(ref("YU", h * n, h * n + n), tl("YI", h))
+            pe([(ref(b[0], j, n, 16), ref("SJb", 128 * j, 128 * j + 128), sm("YC", h), True, True) for j in range(16)])
+            act(ref("YU", h * n, h * n + n), b, F.Copy)
             store(T.yc[:, h * n:h * n + n], ref("YU", h * n, h * n + n, 1, 0, 128, 16))
-            cp(ref("YU", 1024 + h * n, 1024 + h * n + n), L["zf"])
+            act(ref("YU", 1024 + h * n, 1024 + h * n + n), L["zf"], F.Copy)
             store(T.yz[:, h * n:h * n + n], ref("YU", 1024 + h * n, 1024 + h * n + n))
+        mark("kk", h)
         cb = ref(bank(h), 0, 8)
         pe(acc(cb, (Ih, con(8192.0)), (full("I8kn"), lk), (full("I8184"), ov)))
         act(sm("CB", h), cb, F.Copy)
@@ -601,7 +666,7 @@ def build(T, topo, core, rank):
         act(tl("RL", h), y, F.Relu, CL, -1.0)
 
     def bulk(t, h):
-        pg["st"] = BIAS * h
+        mark("hb", h)
         L = tiles(t, h)
         q0, e0 = h * 16 * n, h * 2 * n
         key = tl("KEY", h)
@@ -626,14 +691,20 @@ def build(T, topo, core, rank):
                 o = ref(out[0], out[1] + k, out[2], 16)
                 mm.append((o, ref(R, q0 + k, q0 + 16 * n, 16), full("B32"), not first, False))
                 mm.append((o, ref(D, q0 + k, q0 + 16 * n, 16), full("Bm16"), False, (not first) or k == 15))
-            pe(mm)
+            if len(mm) > 30:
+                pe(mm[:17])
+                pe(mm[17:])
+            else:
+                pe(mm)
         ph, pd = ref(bh_, 0, n), ref(be_, 0, n)
         part("GH", "DH", "RH", e0, 0, n // 2, False)
         part("GH", "DH", "RH", e0, n // 2, n, False)
         sums(ph, "DH", "RH", True)
         act(key, ph, F.Copy)
         he1, he2 = ref("HE", e0, e0 + n), ref("HE", e0 + n, e0 + 2 * n)
+        mark("hm", h)
         tt(tl("HME", h), he1, he2, A.subtract)
+        mark("km", h)
         scan(tl("PM", h), full("RST"), key, 0.0, A.add, A.min)
         mn = ref(bank(h), 0, n, 1, 0, 8)
         pe([(mn, ref("PM", h * n + 15, h * n + n, 16), full("If"), True, True)])
@@ -642,11 +713,13 @@ def build(T, topo, core, rank):
         mx = ref(bank(h), 0, n)
         pe([(mx, mns, g8, True, False), (mx, tl("RL", h), full("BOn"), False, True)])
         tt(tl("OHT", h), key, mx, A.is_equal)
+        mark("eb", h)
         if NE > 0:
             part("GE", "DE", "RE", e0 + n, 0, NE, False)
         if NE < n:
             part("GE", "DE", "RE", e0 + n, NE, n, True)
         sums(pd, "DE", "RE", False)
+        mark("cc", h)
         tt(tl("MT", h), key, pd, A.is_lt)
         mk = ref(bank(h), 0, n)
         pe([(mk, tl("MT", h), full("Ib"), True, True)])
@@ -664,8 +737,9 @@ def build(T, topo, core, rank):
             send("v", t + 1, h, tiles(t + 1, h)["vh"], L["vb"])
         else:
             pe(acc(vo, (full("BOh"), tl("PP", h))))
-            ts(ref("YU", 512 + h * n, 512 + h * n + n), vo, 2048.0, A.add)
+            act(ref("YU", 512 + h * n, 512 + h * n + n), vo, F.Identity, 2048.0)
             store(T.yv[:, h * n:h * n + n], ref("YU", 512 + h * n, 512 + h * n + n, 1, 0, 128, 16))
+        mark("ff", h)
         act(L["fb"], ("ind", L["w4"], sm("TLL", h, 24, 8)), F.Copy)
         if t < NT - 1:
             send("f", t + 1, h, tiles(t + 1, h)["f"], L["fb"])
@@ -673,12 +747,12 @@ def build(T, topo, core, rank):
             store(T.yf[:, h * n:h * n + n], L["fb"])
 
     def scatter(t, h):
-        pg["st"] = BIAS * h
+        mark("sc", h)
         L = tiles(t, h)
         c0 = L["c"][1]
-        for c in range(7, -1, -1):
-            add(pg, "V", 0.12, lambda e, c=c: e.tensor_copy(ap(full("VI")).indirect(ap(ref("OFF", h * 16 + 2 * c, h * 16 + 2 * c + 1))), ap(ref("W", c0 + 16 * c, c0 + 16 * c + 16))),
-                [ref("OFF", h * 16 + 2 * c, h * 16 + 2 * c + 1), ref("W", c0 + 16 * c, c0 + 16 * c + 16)], [full("VI")], tag="scatter")
+        for c in range(3, -1, -1):
+            add(pg, "V", 0.18, lambda e, c=c: e.tensor_copy(ap(full("VI")).indirect(ap(ref("OFF", h * 8 + 2 * c, h * 8 + 2 * c + 2))), ap(ref("W", c0 + 32 * c, c0 + 32 * c + 32))),
+                [ref("OFF", h * 8 + 2 * c, h * 8 + 2 * c + 2), ref("W", c0 + 32 * c, c0 + 32 * c + 32)], [full("VI")], tag="scatter")
 
     front(0, 1)
     sel(full("BOg"), full("BO"), [[1, 128]], A.is_gt, 0.0, 0, -1)

@@ -9,38 +9,39 @@ NT = 5
 XW = 32 + 3 * n
 WW = 4 * n
 MAGIC = 12582912.0
-PRI = {'fr0': 5.1, 'fr1': 10.5, 'qx0': -9.6, 'qx1': -8.0, 'ha0': 12.2, 'ha1': -1.7, 'dd0': -0.6, 'dd1': 5.7, 'h0': -4.5, 'h1': -5.5, 'e0': -9.4, 'e1': 0.6, 'ea0': -3.8, 'ea1': 1.7, 'kk0': -0.1,
-       'kk1': 11.4, 'hb0': -6.6, 'hb1': -5.1, 'hm0': 4.1, 'hm1': -8.8, 'km0': -5.6, 'km1': -2.7, 'eb0': 4.0, 'eb1': -3.3, 'cc0': -4.9, 'cc1': 12.0, 'ff0': 1.5, 'ff1': 16.4, 'sc0': -17.9, 'sc1': -15.7}
-NE = 80
+PRI = {'fr0': 3.4, 'fr1': 10.5, 'qx0': -12.4, 'qx1': -8.0, 'ha0': 6.0, 'ha1': -1.7, 'dd0': -0.6, 'dd1': 4.5, 'h0': -4.1, 'h1': 0.6, 'e0': -9.4, 'e1': 3.2, 'ea0': -3.8, 'ea1': 1.7, 'kk0': -2.7,
+       'kk1': 11.4, 'hb0': -6.6, 'hb1': -5.1, 'hm0': 5.8, 'hm1': -7.9, 'km0': -5.6, 'km1': -1.7, 'eb0': 12.0, 'eb1': -5.3, 'cc0': 3.1, 'cc1': 13.2, 'ff0': 1.5, 'ff1': 11.6, 'sc0': -18.1, 'sc1': -12.0}
+NE = 64
 f4, b2, h2, i4, u2 = "float32", "bfloat16", "float16", "int32", "uint16"
 
 SCRATCH = {
     "PX": ("sbuf", [128, 4096], b2), "VI": ("sbuf", [128, 4096 + 2 * n], f4), "VW": ("sbuf", [128, 2048], i4),
-    "IT": ("sbuf", [128, 1024], i4), "YT": ("sbuf", [128, 2048], f4), "YU": ("sbuf", [128, 2048], f4),
+    "IT": ("sbuf", [128, 2048], i4), "YT": ("sbuf", [128, 2048], f4), "YU": ("sbuf", [128, 2048], f4),
     "XZ": ("sbuf", [128, 10 * XW], b2), "W": ("sbuf", [128, 10 * WW], f4), "VH": ("sbuf", [128, 10 * 8], h2),
     "ZB": ("sbuf", [128, 10 * (32 + n)], b2), "FB": ("sbuf", [128, 10 * n], f4), "VB": ("sbuf", [128, 10 * 8], h2),
     "HE": ("sbuf", [128, 4 * n], f4), "HEL": ("sbuf", [128, 4 * n], u2), "QS": ("sbuf", [128, 16 * n], h2), "QX": ("sbuf", [128, 32 * n], h2),
     "GH": ("sbuf", [128, 32 * n], b2), "GE": ("sbuf", [128, 32 * n], b2), "DH": ("sbuf", [128, 32 * n], h2), "DE": ("sbuf", [128, 32 * n], h2),
     "RH": ("sbuf", [128, 32 * n], h2), "RE": ("sbuf", [128, 32 * n], h2),
-    "OTL": ("sbuf", [128, 16], u2), "AB": ("sbuf", [128, 2 * n], b2), "IND": ("sbuf", [128, 2 * n], h2), "LK": ("sbuf", [128, 16], h2),
+    "OTL": ("sbuf", [128, 16], u2), "AB": ("sbuf", [128, 2 * n], b2), "IND": ("sbuf", [128, 2 * n], h2), "LK": ("sbuf", [128, 16], b2),
     "LSL": ("sbuf", [128, 32], u2), "HI1": ("sbuf", [128, 2 * n], i4), "HI2": ("sbuf", [128, 2 * n], i4), "T1": ("sbuf", [128, 2 * n], f4),
-    "D1": ("sbuf", [128, 16], b2), "OV": ("sbuf", [128, 16], h2), "TLL": ("sbuf", [128, 48], u2), "P1": ("sbuf", [128, 16], b2), "RA": ("sbuf", [128, 80], b2),
-    "KI": ("sbuf", [128, 2 * n], i4), "KJ": ("sbuf", [128, 2 * n], i4), "CB": ("sbuf", [128, 16], b2), "SJb": ("sbuf", [128, 2048], b2), "OK": ("sbuf", [128, 16], f4), "CLB": ("sbuf", [128, 8], f4),
-    "WBs": ("sbuf", [128, 128], b2), "I4kn": ("sbuf", [128, 128], b2), "CH": ("sbuf", [128, 128], b2), "T2": ("sbuf", [128, 2 * n], f4), "FL": ("sbuf", [128, 2 * n], b2), "EQ2": ("sbuf", [128, 2 * n], h2), "OHL": ("sbuf", [128, 2 * n], b2), "RL": ("sbuf", [128, 2 * n], b2),
+    "D1": ("sbuf", [128, 16], b2), "OV": ("sbuf", [128, 16], b2), "TLL": ("sbuf", [128, 48], u2), "P1": ("sbuf", [128, 32], b2), "RA": ("sbuf", [128, 80], b2),
+    "KT": ("sbuf", [128, 2 * n], f4), "KU": ("sbuf", [128, 2 * n], f4), "SP": ("sbuf", [128, 2 * n], f4), "BP": ("sbuf", [128, 8], b2), "CB": ("sbuf", [128, 16], b2), "SJb": ("sbuf", [128, 2048], b2), "OK": ("sbuf", [128, 16], f4), "CLB": ("sbuf", [128, 8], f4),
+    "WBs": ("sbuf", [128, 128], b2), "I4kn": ("sbuf", [128, 128], b2), "CH": ("sbuf", [128, 128], b2), "T2": ("sbuf", [128, 2 * n], f4), "FL": ("sbuf", [128, 2 * n], b2), "EQ2": ("sbuf", [128, 2 * n], h2), "OHL": ("sbuf", [128, 2 * n], b2),
     "VS": ("sbuf", [128, 2 * n], f4), "VR": ("sbuf", [128, 2 * n], f4), "EQ": ("sbuf", [128, 2 * n], b2),
-    "W0": ("sbuf", [128, 16], h2), "O2": ("sbuf", [128, 16], f4), "OFF": ("sbuf", [128, 32], u2),
+    "W0": ("sbuf", [128, 16], b2), "O2": ("sbuf", [128, 16], f4), "OFF": ("sbuf", [128, 32], u2),
     "HME": ("sbuf", [128, 2 * n], f4), "KEY": ("sbuf", [128, 2 * n], f4), "MT": ("sbuf", [128, 2 * n], b2), "MM": ("sbuf", [128, 2 * n], f4),
     "PM": ("sbuf", [128, 2 * n], f4), "MN": ("sbuf", [128, 2 * n], f4), "OHT": ("sbuf", [128, 2 * n], b2), "CF": ("sbuf", [128, 2 * n], f4), "PP": ("sbuf", [128, 2 * n], h2),
-    "I16b": ("sbuf", [128, 128], b2), "I8184": ("sbuf", [128, 128], h2), "I8k": ("sbuf", [128, 128], h2), "I8kn": ("sbuf", [128, 128], h2), "BO613": ("sbuf", [128, 128], h2), "C256": ("sbuf", [128, n], h2),
+    "I16b": ("sbuf", [128, 128], b2), "I8k": ("sbuf", [128, 128], b2), "I8kn": ("sbuf", [128, 128], b2), "BO613": ("sbuf", [128, 128], h2), "C256": ("sbuf", [128, n], h2),
     "If": ("sbuf", [128, 128], f4), "Ib": ("sbuf", [128, 128], b2), "Ih": ("sbuf", [128, 128], h2), "Inb": ("sbuf", [128, 128], b2), "Ihalf": ("sbuf", [128, 128], b2),
-    "Sb": ("sbuf", [128, 128], b2), "Sh": ("sbuf", [128, 128], h2), "Sh100": ("sbuf", [128, 128], h2), "In": ("sbuf", [128, 128], h2), "I2n": ("sbuf", [128, 128], h2),
-    "Ip100": ("sbuf", [128, 128], h2), "Im100": ("sbuf", [128, 128], h2), "I8": ("sbuf", [128, 128], h2),
-    "G2n": ("sbuf", [128, 128], h2), "Gn": ("sbuf", [128, 128], h2), "G0": ("sbuf", [128, 128], h2),
-    "ONE": ("sbuf", [128, 128], f4), "G8": ("sbuf", [128, 128], f4), "BO": ("sbuf", [128, 128], b2), "BOn": ("sbuf", [128, 128], b2), "BOh": ("sbuf", [128, 128], h2), "BOg": ("sbuf", [128, 128], b2), "WB": ("sbuf", [128, 128], b2),
+    "Sb": ("sbuf", [128, 128], b2), "Sb100": ("sbuf", [128, 128], b2), "In": ("sbuf", [128, 128], b2), "I2n": ("sbuf", [128, 128], b2),
+    "Imh": ("sbuf", [128, 128], b2), "I7h": ("sbuf", [128, 128], b2), "I4k": ("sbuf", [128, 128], f4),
+    "Ip100": ("sbuf", [128, 128], b2), "Im100": ("sbuf", [128, 128], b2),
+    "Gn": ("sbuf", [128, 128], b2), "G0": ("sbuf", [128, 128], b2),
+    "ONE": ("sbuf", [128, 128], f4), "G8": ("sbuf", [128, 128], f4), "BO": ("sbuf", [128, 128], b2), "BOh": ("sbuf", [128, 128], h2), "BOg": ("sbuf", [128, 128], b2), "WB": ("sbuf", [128, 128], b2),
     "Bh": ("sbuf", [128, 144], h2), "B32": ("sbuf", [128, 8], h2), "Bm16": ("sbuf", [128, 8], h2),
     "SJ": ("sbuf", [128, 2048], h2), "LTJ": ("sbuf", [128, 2048], b2), "PI": ("sbuf", [128, 32], i4), "PC": ("sbuf", [128, 16], f4),
-    "OJ": ("sbuf", [128, 16], f4),  "IJ": ("sbuf", [128, 16], f4), "CMI": ("sbuf", [128, 8], f4), "CM": ("sbuf", [128, 24], h2), "CMm": ("sbuf", [128, 16], h2),
-    "CON": ("sbuf", [128, 64], h2), "KC": ("sbuf", [128, 128], b2), "MK": ("sbuf", [128, 16 * n], b2), "MF": ("sbuf", [128, n], f4), "RST": ("sbuf", [128, 128], f4),
+    "OJ": ("sbuf", [128, 16], f4),  "IJ": ("sbuf", [128, 16], f4), "CMI": ("sbuf", [128, 8], f4), "CM": ("sbuf", [128, 32], h2), "CMm": ("sbuf", [128, 16], h2),
+    "CON": ("sbuf", [128, 80], b2), "O2V": ("sbuf", [128, 32], b2), "KC": ("sbuf", [128, 128], b2), "MK": ("sbuf", [128, 16 * n], b2), "MF": ("sbuf", [128, n], f4), "RST": ("sbuf", [128, 128], f4),
     "CQ": ("sbuf", [128, 128], b2), "ON": ("sbuf", [128, 128], b2), "WT": ("sbuf", [128, 2], i4), "WTf": ("sbuf", [128, 8], f4),
     "VZ": ("sbuf", [128, 512], i4), "VZi": ("sbuf", [128, 512], i4), "VZh": ("sbuf", [128, 768], h2), "FI": ("sbuf", [128, 256], i4), "YC": ("sbuf", [128, 16], b2),
 }
@@ -74,10 +75,7 @@ def touch(pg, o, r, wr):
                 elif o["q"] == "P":
                     o["ord"].add(p)
             elif over and (wr or aw):
-                if aw or ops[p]["q"] != o["q"]:
-                    o["dep"].add(p)
-                else:
-                    o["ord"].add(p)
+                o["dep"].add(p)
         if wr and a0 >= c0 and a1 <= c1 and p != o["i"] and not psum and r[3] == 1 and r[6] == 1:
             continue
         keep.append(a)
@@ -415,6 +413,7 @@ def build(T, topo, core, rank):
             fn = lambda e: e.iota(ap(out), pat, base, cm)
         return add(pg, "G", 0.2 + 2 * CY * cnt(out), fn, [], [out], tag="iota")
 
+    iota0 = lambda out: iota(out, [[0, cnt(out)]], 0, 0, True)
     fill(full("ONE"), 1.0)
     sel(full("G8"), full("ONE"), [[1, 128]], A.is_ge, 0.0, 0, -16)
     sel(full("G8"), full("G8"), [[-1, 128]], A.is_ge, 0.0, 15, 16)
@@ -427,7 +426,6 @@ def build(T, topo, core, rank):
     bk = bank(0)
     pe([(ref(bk, 0, 128), g8, g8, True, True)])
     cp(full("BO"), ref(bk, 0, 128))
-    act(full("BOn"), full("BO"), F.Copy, 0.0, -1.0)
     cp(full("BOh"), full("BO"))
     cp(full("Ib"), full("If"))
     cp(full("Ih"), full("If"))
@@ -436,7 +434,9 @@ def build(T, topo, core, rank):
     act(full("I16b"), full("If"), F.Copy, 0.0, 16.0)
     ts(ref("PI", 16, 17), ref("PI", 0, 1), 15, A.bitwise_and)
     ts(ref("PI", 24, 25), ref("PI", 0, 1), 1, A.bitwise_and)
-    pm, sg = ref("PC", 0, 1), ref("PC", 4, 5)
+    pm, sg, sgn, pmh = ref("PC", 0, 1), ref("PC", 4, 5), ref("PC", 8, 9), ref("PC", 12, 13)
+    ts(sgn, ref("PI", 24, 25), -2.0, A.mult, 1.0 + n, A.add)
+    ts(pmh, ref("PI", 16, 17), -7.5, A.add)
     cp(pm, ref("PI", 16, 17))
     ts(sg, ref("PI", 24, 25), -2.0, A.mult, 1.0, A.add)
     cp(ref("WTf", 0, 2), full("WT"))
@@ -444,9 +444,8 @@ def build(T, topo, core, rank):
     act(full("WB"), full("BO"), F.Copy, 0.0, wcol)
     fill(full("Bh"), 0.0)
     cp(ref("Bh", 15, 143, 16), ref("BO", 0, 128, 16))
-    fill(ref("CLB", 0, 4), 8192.0)
-    fill(ref("CLB", 4, 8), -65536.0)
-    CL, HB = ref("CLB", 0, 1), ref("CLB", 4, 5)
+    fill(full("CLB"), -65536.0)
+    HB = ref("CLB", 0, 1)
     act(full("WBs"), full("WB"), F.Copy, 0.0, 1.0 / 4096)
     act(full("I4kn"), full("If"), F.Copy, 0.0, -4096.0)
     fill(ref("CH", 0, 128, 1, 0, 64), -0.5 / 64)
@@ -460,37 +459,40 @@ def build(T, topo, core, rank):
     for j in range(16):
         act(ref("SJb", 128 * j, 128 * j + 128), full("BO"), F.Copy, 0.0, ref("OK", j, j + 1))
     ts(ref("CM", 0, 8), full("CMI"), pm, A.add)
-    ts(ref("CM", 8, 16), ref("CM", 0, 8), float(2 * n), A.add)
-    ts(ref("CM", 16, 24), ref("CM", 0, 8), float(3 * n), A.add)
+    ts(ref("CM", 8, 16), full("CMI"), pm, A.add)
+    ts(ref("CM", 16, 24), ref("CM", 0, 8), float(2 * n), A.add)
+    ts(ref("CM", 24, 32), ref("CM", 0, 8), float(3 * n), A.add)
+    iota(ref("CON", 56, 72), [[0, 16]], -100, 0, True)
     for h in range(2):
         ts(sm("CMm", h), ref("CM", 0, 8), float(n * h), A.add)
-    consts = (-9.0, 8192.0, -4096.0, 2048.0, -100.0, 1.0, 100.0)
+    consts = (-9, -4096, 2048, -100, 1, 100)
     for i, c in enumerate(consts):
-        fill(ref("CON", 8 * i, 8 * i + 8), c)
-    con = lambda c: ref("CON", 8 * consts.index(c), 8 * consts.index(c) + 8)
-    for nm, src, c in (("In", "Ih", float(n)), ("I2n", "Ih", float(2 * n)), ("Ip100", "Ih", 100.0), ("Im100", "Ih", -100.0), ("I8", "Ih", 8.0),
-                       ("I8k", "Ih", 8192.0), ("I8kn", "Ih", -8192.0), ("BO613", "BOh", 613.0), ("I8184", "Ih", -8184.0)):
-        ts(full(nm), full(src), c, A.mult)
-    ts(full("G0"), full("Ih"), sg, A.mult)
-    tt(full("Gn"), full("G0"), full("In"), A.add)
-    tt(full("G2n"), full("G0"), full("I2n"), A.add)
+        iota(ref("CON", 8 * i, 8 * i + 8), [[0, 8]], c, 0, True)
+    con = lambda c: ref("CON", 8 * consts.index(int(c)), 8 * consts.index(int(c)) + 8)
+    ts(full("BO613"), full("BOh"), 613.0, A.mult)
+    for nm, c in (("In", float(n)), ("I2n", float(2 * n)), ("I8k", 8192.0), ("Im100", -100.0), ("Ip100", 100.0), ("I8kn", -8192.0), ("Imh", -0.5), ("I7h", 7.5)):
+        act(full(nm), full("If"), F.Copy, 0.0, c)
+    act(full("G0"), full("If"), F.Copy, 0.0, sg)
+    act(full("Gn"), full("If"), F.Copy, 0.0, sgn)
+    act(full("BP"), ref("BO", 0, 128, 16), F.Copy, 0.0, -1048576.0)
     act(ref("Sb", 0, 128, 2), ref("If", 1, 128, 2), F.Copy)
     act(ref("Sb", 1, 128, 2), ref("If", 0, 128, 2), F.Copy)
-    cp(full("Sh"), full("Sb"))
-    ts(full("Sh100"), full("Sb"), 100.0, A.mult)
+    act(full("Sb100"), full("Sb"), F.Copy, 0.0, 100.0)
+    act(full("I4k"), full("If"), F.Copy, 0.0, 4096.0)
     fill(full("ON"), 1.0)
     fill(full("CQ"), -0.25 / 128)
     iota(full("MK"), [[0, 16 * n]], 1, 0, True)
     sel(full("MK"), full("MK"), [[0, n], [1, 16]], A.not_equal, 0.0, 0, 0)
-    fill(full("MF"), 1.0)
-    fill(ref("MF", 0, n, 16), 0.0)
-    fill(full("RST"), 0.0)
-    fill(ref("RST", 0, 128, 16), 1048576.0)
+    iota(full("MF"), [[0, n]], 1, 0, True)
+    sel(full("MF"), full("MF"), [[0, n // 16], [1, 16]], A.not_equal, 0.0, 0, 0)
+    iota(full("RST"), [[0, 128]], 0, 0, True)
+    sel(full("RST"), full("RST"), [[0, 8], [1, 16]], A.not_equal, 1048576.0, 0, 0)
     fill(full("QS"), 0.0)
     fill(full("C256"), 256.0)
-    fill(full("VS"), 0.0)
+    iota(full("VS"), [[0, 2 * n]], 0, 0, True)
+    iota(full("SP"), [[0, 2 * n]], 0, 0, True)
     for k in range(8):
-        fill(ref("ZB", k * (32 + n) + 24, k * (32 + n) + 32), 0.0)
+        iota0(ref("ZB", k * (32 + n) + 24, k * (32 + n) + 32))
 
     def ots(out, tile, base="Bh", first=(), last=()):
         prs = list(first)
@@ -519,7 +521,7 @@ def build(T, topo, core, rank):
         cp(ref("W", h * WW + n, h * WW + 2 * n), ref("FI", h * n, h * n + n))
     for c in range(2):
         x = ref("VW", 1024 * c, 1024 * c + 1024)
-        it = full("IT")
+        it = ref("IT", 1024 * c, 1024 * c + 1024)
         ts(it, x, 4095, A.bitwise_and)
         cp(ref("VI", 1024 * c, 1024 * c + 1024), it)
         ts(x, x, 12, A.arith_shift_right)
@@ -560,12 +562,12 @@ def build(T, topo, core, rank):
         pe([(vk, full("BO613"), full("C256"), True, False)]
            + [(ref(vk[0], j, n, 16), ref("SJ", 128 * j, 128 * j + 128), L["vh"], False, j == 15) for j in range(16)])
         ct = ref(bank(h), 0, 8)
-        pe(ots(ct, tl("IND", h), "Bh", [(full("Ih"), con(-9.0))], [(full("Inb"), L["cnt"](1))]))
+        pe(ots(ct, tl("IND", h), "Bh", [(full("Ib"), con(-9.0))], [(full("Inb"), L["cnt"](1))]))
         lk = sm("LK", h)
         ts(lk, ct, -0.5, A.is_ge)
         b = bank(h)
-        pe(acc(ref(b, 0, 8), (full("Ih"), ref("CM", 0, 8)), (full("In"), lk)) + acc(ref(b, 8, 16), (full("Ih"), ref("CM", 0, 8)), (full("I2n"), lk))
-           + acc(ref(b, 16, 24), (full("Ih"), L["vh"]), (full("Ih"), con(-4096.0)), (full("I8k"), lk)))
+        pe([(ref(b, 0, 16), full("Ih"), ref("CM", 0, 16), True, False), (ref(b, 0, 8), full("In"), lk, False, False), (ref(b, 8, 16), full("I2n"), lk, False, True)]
+           + acc(ref(b, 16, 24), (full("Ih"), L["vh"]), (full("Ib"), con(-4096.0)), (full("I8k"), lk)))
         cp(sm("LSL", h, 16, 0, 16), ref(b, 0, 16))
         act(ref("VS", h * n, h * n + n, 16), ref(b, 16, 24), F.Relu, 0.0, 613.0)
         q0 = h * 16 * n
@@ -599,12 +601,12 @@ def build(T, topo, core, rank):
         L = tiles(t, h)
         lk = sm("LK", h)
         du = ref(bank(h), 0, 8)
-        m3 = acc(du, *([(full("Ih"), con(100.0)), (full("Im100"), lk)] + [(ref("LTJ", 128 * j, 128 * j + 128), ref("EQ", h * n + j, h * n + n, 16)) for j in range(16)]))
+        m3 = acc(du, *([(full("Ib"), con(100.0)), (full("Im100"), lk)] + [(ref("LTJ", 128 * j, 128 * j + 128), ref("EQ", h * n + j, h * n + n, 16)) for j in range(16)]))
         m3[-1] = m3[-1][:4] + (False,)
         pe(m3 + [(ref(du[0], 1, 8, 2), ref("Bh", 15 - j, 143 - j), ref("EQ2", h * n + 16 + j, h * n + n, 32), False, j == 15) for j in range(16)])
         ts(sm("W0", h), du, 0.5, A.is_lt)
         vd = ref(bank(h), 0, 8)
-        pe(acc(vd, (full("Ih"), con(2048.0)), (full("Ih"), sm("CMm", h)), (full("I8kn"), sm("W0", h))))
+        pe(acc(vd, (full("Ib"), con(2048.0)), (full("Ih"), sm("CMm", h)), (full("I8kn"), sm("W0", h))))
         tt(sm("O2", h), L["vh"], vd, A.max)
         ts(sm("OFF", h), sm("O2", h), 2048.0, A.add)
 
@@ -612,7 +614,7 @@ def build(T, topo, core, rank):
         mark("ea", h)
         L = tiles(t, h)
         lk, d1, ov = sm("LK", h), sm("D1", h), sm("OV", h)
-        Ih, Ib, Sh, Sb, Ip, Im = full("Ih"), full("Ib"), full("Sh"), full("Sb"), full("Ip100"), full("Im100")
+        Ih, Ib, Sb, Ip, Im = full("Ih"), full("Ib"), full("Sb"), full("Ip100"), full("Im100")
         hz = ref(bank(h), 0, n)
         pe(acc(hz, (full("Ihalf"), L["x"]), (full("Ihalf"), L["z"]), (full("CQ"), full("ON"))))
         act(tl("T1", h), hz, F.Identity, MAGIC)
@@ -621,31 +623,33 @@ def build(T, topo, core, rank):
         pe(acc(dp, (Ib, L["cnt"](2)), (Im, lk)))
         act(d1, dp, F.Relu)
         po = ref(bank(h), 0, 8)
-        pe(acc(po, (Ib, d1), (full("Sh100"), lk)))
+        pe(acc(po, (Ib, d1), (full("Sb100"), lk)))
         ts(ov, po, 101.5, A.is_ge)
         b = bank(h)
-        pe(acc(ref(b, 0, 8), (Ih, ref("CM", 0, 8)), (full("I2n"), lk), (full("G2n"), ov))
-           + acc(ref(b, 8, 16), (Ih, ref("CM", 8, 16)), (full("In"), lk), (full("Gn"), ov))
-           + acc(ref(b, 16, 24), (Ih, ref("CM", 16, 24)), (full("G0"), ov)))
+        pe([(ref(b, 0, 24), Ih, ref("CM", 8, 32), True, False)]
+           + [(ref(b, c, c + 8), full(m), v, False, c == 16) for c, m, v in ((0, "I2n", lk), (0, "I2n", ov), (0, "G0", ov), (8, "In", lk), (8, "Gn", ov), (16, "G0", ov))])
         cp(sm("TLL", h, 24, 0, 24), ref(b, 0, 24))
         act(L["zf"], ("ind", L["xzh"], sm("TLL", h, 24)), F.Copy)
-        pp = ref(bank(h), 0, 8)
-        pe(acc(pp, (Ih, lk), (full("Inb"), L["cnt"](1))))
-        act(sm("P1", h), pp, F.Abs)
         b = bank(h)
-        p1, ca = sm("P1", h), L["cnt"](0)
-        pe(acc(ref(b, 0, 8), (Ib, ca), (Ih, lk), (Im, ov)) + acc(ref(b, 8, 16), (Sb, ca), (Sh, lk), (Ip, ov), (Ih, con(-100.0)))
-           + acc(ref(b, 16, 24), (Ib, p1), (Im, ov)) + acc(ref(b, 24, 32), (Sb, p1), (Ip, ov), (Ih, con(-100.0))) + acc(ref(b, 32, 40), (Ib, d1), (Im, ov)))
+        pe([(ref(b, 0, 16), Ib, ref(L["cnt"](0)[0], L["cnt"](0)[1], L["cnt"](1)[2]), True, False), (ref(b, 0, 8), Ib, lk, False, False), (ref(b, 8, 16), full("Inb"), lk, False, True)])
+        ap_ = sm("P1", h, 16, 0, 16)
+        act(ap_, ref(b, 0, 16), F.Abs)
+        act(sm("O2V", h, 16), ov, F.Copy)
+        act(sm("O2V", h, 16, 8), ov, F.Copy)
+        oo = sm("O2V", h, 16, 0, 16)
+        b = bank(h)
+        pe(acc(ref(b, 0, 16), (Ib, ap_), (Im, oo)) + acc(ref(b, 16, 32), (Sb, ap_), (Ip, oo), (Ib, ref("CON", 56, 72))) + acc(ref(b, 32, 40), (Ib, d1), (Im, ov)))
         ra = lambda j: sm("RA", h, 40, 8 * j)
+        ra2 = lambda j: sm("RA", h, 40, 16 * j, 16)
         act(sm("RA", h, 40, 0, 40), ref(b, 0, 40), F.Relu)
         b = bank(h)
         if t < NT - 1:
-            pe(acc(ref(b, 0, 8), (Ib, ra(0)), (Ib, ra(1))) + acc(ref(b, 8, 16), (Ib, ra(2)), (Ib, ra(3))) + acc(ref(b, 16, 24), (Ib, ra(4)), (Ih, con(1.0))))
+            pe(acc(ref(b, 0, 16), (Ib, ra2(0)), (Ib, ra2(1))) + acc(ref(b, 16, 24), (Ib, ra(4)), (Ib, con(1.0))))
             act(L["zc"], ref(b, 0, 24), F.Copy)
             send("z", t + 1, h, tiles(t + 1, h)["land"], L["zb"])
         else:
             i16 = full("I16b")
-            pe(acc(ref(b, 0, 8), (i16, ra(0)), (i16, ra(1)), (Ib, ra(4))))
+            pe(acc(ref(b, 0, 8), (i16, ra(0)), (i16, ra(2)), (Ib, ra(4))))
             act(sm("YC", h), ref(b, 0, 8), F.Copy)
             b = ref(bank(h), 0, n)
             pe([(ref(b[0], j, n, 16), ref("SJb", 128 * j, 128 * j + 128), sm("YC", h), True, True) for j in range(16)])
@@ -655,15 +659,15 @@ def build(T, topo, core, rank):
             store(T.yz[:, h * n:h * n + n], ref("YU", 1024 + h * n, 1024 + h * n + n))
         mark("kk", h)
         cb = ref(bank(h), 0, 8)
-        pe(acc(cb, (Ih, con(8192.0)), (full("I8kn"), lk), (full("I8184"), ov)))
-        act(sm("CB", h), cb, F.Copy)
+        pe(acc(cb, (full("Imh"), lk), (full("I7h"), ov)))
+        act(sm("CB", h), cb, F.Identity, t - 7.0)
         y = ref(bank(h), 0, n)
         pe([(y, full("BO"), L["zf"], True, False)]
            + [(ref(y[0], j, n, 16), ref("SJb", 128 * j, 128 * j + 128), sm("CB", h), False, j == 15) for j in range(16)])
-        ts(tl("KI", h), y, float(t), A.add)
-        ts(tl("KJ", h), tl("KI", h), 8192 + 15, A.bitwise_and)
-        ts(tl("OHL", h), tl("KJ", h), pm, A.is_equal)
-        act(tl("RL", h), y, F.Relu, CL, -1.0)
+        act(tl("KT", h), y, F.Identity, MAGIC, 1.0 / 16)
+        act(tl("KU", h), tl("KT", h), F.Identity, -MAGIC)
+        act(tl("KT", h), tl("KU", h), F.Identity, pmh, 16.0)
+        tt(tl("OHL", h), tl("KT", h), y, A.is_equal)
 
     def bulk(t, h):
         mark("hb", h)
@@ -706,13 +710,11 @@ def build(T, topo, core, rank):
         tt(tl("HME", h), he1, he2, A.subtract)
         mark("km", h)
         scan(tl("PM", h), full("RST"), key, 0.0, A.add, A.min)
-        mn = ref(bank(h), 0, n, 1, 0, 8)
-        pe([(mn, ref("PM", h * n + 15, h * n + n, 16), full("If"), True, True)])
-        mns = ref("MN", h * n, h * n + n, 1, 0, 8)
-        act(mns, mn, F.Copy)
-        mx = ref(bank(h), 0, n)
-        pe([(mx, mns, g8, True, False), (mx, tl("RL", h), full("BOn"), False, True)])
-        tt(tl("OHT", h), key, mx, A.is_equal)
+        mx = ref(bank(h), 0, 8)
+        pe([(mx, tl("OHL", h), full("BP"), True, True)])
+        tt(ref("SP", h * n, h * n + n, 16), ref("PM", h * n + 15, h * n + n, 16), mx, A.add)
+        scan(tl("MN", h), full("MF"), tl("SP", h), 0.0, A.mult, A.add)
+        tt(tl("OHT", h), tl("MN", h), ph, A.is_equal)
         mark("eb", h)
         if NE > 0:
             part("GE", "DE", "RE", e0 + n, 0, NE, False)
@@ -774,8 +776,15 @@ def build(T, topo, core, rank):
         if t < NT - 1:
             front(t + 1, 1)
             front(t + 1, 0)
-    for c in range(4):
+    pg["st"] = ""
+    for c in (3, 0, 1, 2):
         a, b = 512 * c, 512 * c + 512
+        if c == 3:
+            yb = ref(bank(0), 0, 512)
+            pe(acc(yb, (full("If"), ref("VI", a, b)), (full("I4k"), ref("VI", 2048 + a, 2048 + b))))
+            act(ref("YT", a, b), yb, F.Copy)
+            store(T.yw[:, a:b], ref("YT", a, b))
+            continue
         act(ref("YT", a, b), ref("VI", 2048 + a, 2048 + b), F.Copy, 0.0, 4096.0)
         tt(ref("YT", a, b), ref("YT", a, b), ref("VI", a, b), A.add)
         store(T.yw[:, a:b], ref("YT", a, b))

import numpy as np
from concourse.bass import DstId, RemoteDMATransfer
from concourse.mybir import dt, AluOpType, AxisListType, ActivationFunctionType

A = AluOpType
F = ActivationFunctionType
n = 128
NT = 5
XW = 32 + 3 * n
WW = 4 * n
MAGIC = 12582912.0
PRI = {'fr0': 3.4, 'fr1': 10.5, 'qx0': -12.4, 'qx1': -8.0, 'ha0': 6.0, 'ha1': -1.7, 'dd0': -0.6, 'dd1': 4.5, 'h0': -4.1, 'h1': 0.6, 'e0': -9.4, 'e1': 3.2, 'ea0': -3.8, 'ea1': 1.7, 'kk0': -2.7,
       'kk1': 11.4, 'hb0': -6.6, 'hb1': -5.1, 'hm0': 5.8, 'hm1': -7.9, 'km0': -5.6, 'km1': -1.7, 'eb0': 12.0, 'eb1': -5.3, 'cc0': 3.1, 'cc1': 13.2, 'ff0': 1.5, 'ff1': 11.6, 'sc0': -18.1, 'sc1': -12.0}
NE = 64
f4, b2, h2, i4, u2 = "float32", "bfloat16", "float16", "int32", "uint16"

SCRATCH = {
    "PX": ("sbuf", [128, 4096], b2), "VI": ("sbuf", [128, 4096 + 2 * n], f4), "VW": ("sbuf", [128, 2048], i4),
    "IT": ("sbuf", [128, 2048], i4), "YT": ("sbuf", [128, 2048], f4), "YU": ("sbuf", [128, 2048], f4),
    "XZ": ("sbuf", [128, 10 * XW], b2), "W": ("sbuf", [128, 10 * WW], f4), "VH": ("sbuf", [128, 10 * 8], h2),
    "ZB": ("sbuf", [128, 10 * (32 + n)], b2), "FB": ("sbuf", [128, 10 * n], f4), "VB": ("sbuf", [128, 10 * 8], h2),
    "HE": ("sbuf", [128, 4 * n], f4), "HEL": ("sbuf", [128, 4 * n], u2), "QS": ("sbuf", [128, 16 * n], h2), "QX": ("sbuf", [128, 32 * n], h2),
    "GH": ("sbuf", [128, 32 * n], b2), "GE": ("sbuf", [128, 32 * n], b2), "DH": ("sbuf", [128, 32 * n], h2), "DE": ("sbuf", [128, 32 * n], h2),
    "RH": ("sbuf", [128, 32 * n], h2), "RE": ("sbuf", [128, 32 * n], h2),
    "OTL": ("sbuf", [128, 16], u2), "AB": ("sbuf", [128, 2 * n], b2), "IND": ("sbuf", [128, 2 * n], h2), "LK": ("sbuf", [128, 16], b2),
    "LSL": ("sbuf", [128, 32], u2), "HI1": ("sbuf", [128, 2 * n], i4), "HI2": ("sbuf", [128, 2 * n], i4), "T1": ("sbuf", [128, 2 * n], f4),
    "D1": ("sbuf", [128, 16], b2), "OV": ("sbuf", [128, 16], b2), "TLL": ("sbuf", [128, 48], u2), "P1": ("sbuf", [128, 32], b2), "RA": ("sbuf", [128, 80], b2),
    "KT": ("sbuf", [128, 2 * n], f4), "KU": ("sbuf", [128, 2 * n], f4), "SP": ("sbuf", [128, 2 * n], f4), "BP": ("sbuf", [128, 8], b2), "CB": ("sbuf", [128, 16], b2), "SJb": ("sbuf", [128, 2048], b2), "OK": ("sbuf", [128, 16], f4), "CLB": ("sbuf", [128, 8], f4),
    "WBs": ("sbuf", [128, 128], b2), "I4kn": ("sbuf", [128, 128], b2), "CH": ("sbuf", [128, 128], b2), "T2": ("sbuf", [128, 2 * n], f4), "FL": ("sbuf", [128, 2 * n], b2), "EQ2": ("sbuf", [128, 2 * n], h2), "OHL": ("sbuf", [128, 2 * n], b2),
    "VS": ("sbuf", [128, 2 * n], f4), "VR": ("sbuf", [128, 2 * n], f4), "EQ": ("sbuf", [128, 2 * n], b2),
    "W0": ("sbuf", [128, 16], b2), "O2": ("sbuf", [128, 16], f4), "OFF": ("sbuf", [128, 32], u2),
    "HME": ("sbuf", [128, 2 * n], f4), "KEY": ("sbuf", [128, 2 * n], f4), "MT": ("sbuf", [128, 2 * n], b2), "MM": ("sbuf", [128, 2 * n], f4),
    "PM": ("sbuf", [128, 2 * n], f4), "MN": ("sbuf", [128, 2 * n], f4), "OHT": ("sbuf", [128, 2 * n], b2), "CF": ("sbuf", [128, 2 * n], f4), "PP": ("sbuf", [128, 2 * n], h2),
    "I16b": ("sbuf", [128, 128], b2), "I8k": ("sbuf", [128, 128], b2), "I8kn": ("sbuf", [128, 128], b2), "BO613": ("sbuf", [128, 128], h2), "C256": ("sbuf", [128, n], h2),
    "If": ("sbuf", [128, 128], f4), "Ib": ("sbuf", [128, 128], b2), "Ih": ("sbuf", [128, 128], h2), "Inb": ("sbuf", [128, 128], b2), "Ihalf": ("sbuf", [128, 128], b2),
    "Sb": ("sbuf", [128, 128], b2), "Sb100": ("sbuf", [128, 128], b2), "In": ("sbuf", [128, 128], b2), "I2n": ("sbuf", [128, 128], b2),
    "Imh": ("sbuf", [128, 128], b2), "I7h": ("sbuf", [128, 128], b2), "I4k": ("sbuf", [128, 128], f4),
    "Ip100": ("sbuf", [128, 128], b2), "Im100": ("sbuf", [128, 128], b2),
    "Gn": ("sbuf", [128, 128], b2), "G0": ("sbuf", [128, 128], b2),
    "ONE": ("sbuf", [128, 128], f4), "G8": ("sbuf", [128, 128], f4), "BO": ("sbuf", [128, 128], b2), "BOh": ("sbuf", [128, 128], h2), "BOg": ("sbuf", [128, 128], b2), "WB": ("sbuf", [128, 128], b2),
    "Bh": ("sbuf", [128, 144], h2), "B32": ("sbuf", [128, 8], h2), "Bm16": ("sbuf", [128, 8], h2),
    "SJ": ("sbuf", [128, 2048], h2), "LTJ": ("sbuf", [128, 2048], b2), "PI": ("sbuf", [128, 32], i4), "PC": ("sbuf", [128, 16], f4),
    "OJ": ("sbuf", [128, 16], f4),  "IJ": ("sbuf", [128, 16], f4), "CMI": ("sbuf", [128, 8], f4), "CM": ("sbuf", [128, 32], h2), "CMm": ("sbuf", [128, 16], h2),
    "CON": ("sbuf", [128, 80], b2), "O2V": ("sbuf", [128, 32], b2), "KC": ("sbuf", [128, 128], b2), "MK": ("sbuf", [128, 16 * n], b2), "MF": ("sbuf", [128, n], f4), "RST": ("sbuf", [128, 128], f4),
    "CQ": ("sbuf", [128, 128], b2), "ON": ("sbuf", [128, 128], b2), "WT": ("sbuf", [128, 2], i4), "WTf": ("sbuf", [128, 8], f4),
    "VZ": ("sbuf", [128, 512], i4), "VZi": ("sbuf", [128, 512], i4), "VZh": ("sbuf", [128, 768], h2), "FI": ("sbuf", [128, 256], i4), "YC": ("sbuf", [128, 16], b2),
}
for _b in range(8):
    SCRATCH["b%d" % _b] = ("psum", [128, 512], f4)
LOADS = ["px0", "px1", "vw0", "vw1", "z0", "z1", "f0", "v0", "d0", "wt", "kap"]
SEMAPHORES = ["V", "S", "P", "G", "out", "ls"] + ["ld_" + x for x in LOADS] + ["r%s_%d_%d" % (k, t, h) for k in "zfv" for t in range(1, NT) for h in range(2)]


def ref(name, c0, c1, step=1, p0=0, p1=128, pstep=1):
    return (name, c0, c1, step, p0, p1, pstep)


def new_prog():
    return {"ops": [], "acc": {}, "rr": [0], "st": "", "bmap": {}}


def touch(pg, o, r, wr):
    name, c0, c1 = r[0], r[1], r[2]
    lst = pg["acc"].setdefault(name, [])
    psum = name[0] == "b" and name[1:].isdigit()
    ops = pg["ops"]
    keep = []
    for a in lst:
        p, a0, a1, aw = a
        over = a0 < c1 and c0 < a1
        if p != o["i"]:
            if psum:
                if ops[p]["q"] != o["q"]:
                    o["dep"].add(p)
                elif o["q"] == "P":
                    o["ord"].add(p)
            elif over and (wr or aw):
                o["dep"].add(p)
        if wr and a0 >= c0 and a1 <= c1 and p != o["i"] and not psum and r[3] == 1 and r[6] == 1:
            continue
        keep.append(a)
    if psum and len(keep) > 24:
        keep = keep[-24:]
    keep.append((o["i"], c0, c1, wr))
    pg["acc"][name] = keep


def add(pg, q, cost, fn, rd, wr, sem=None, val=1, after=(), lat=0.0, tag=""):
    o = {"i": len(pg["ops"]), "q": q, "cost": cost, "fn": fn, "dep": set(after), "ord": set(), "sem": sem, "val": val, "lat": lat, "send": None, "tag": tag, "st": pg["st"], "wake": WAKE}
    pg["ops"].append(o)
    for r in rd:
        touch(pg, o, r, False)
    for r in wr:
        touch(pg, o, r, True)
    o["tiles"] = sorted(set(r[0] for r in list(rd) + list(wr) if r[0][0] == "b" and r[0][1:].isdigit()))
    o["dyn"] = set()
    return o["i"]


WAKE = 0.10
GC = 1.5
PEC = 0.00055
CY = 0.00083
LNK = 1.6
FIX = {"V": 0.03, "S": 0.04, "P": 0.03, "G": 0.05, "Y": 0.05}


def schedule(pg):
    ops = pg["ops"]
    N_ = len(ops)
    succ = [[] for _ in ops]
    cnt = [0] * N_
    for o in ops:
        ps = set(o["dep"]) | o["ord"]
        if o["send"] is not None:
            ps.add(o["send"])
        cnt[o["i"]] = len(ps)
        for p in ps:
            succ[p].append(o["i"])
    pri = [0.0] * N_
    for o in reversed(ops):
        i = o["i"]
        pri[i] = max([pri[s] for s in succ[i]] + [0.0]) + o["cost"] + o["lat"] + WAKE
    for o in ops:
        pri[o["i"]] += PRI.get(o["st"], 0.0)
    uses, first = {}, {}
    for o in ops:
        for tname in o["tiles"]:
            if tname not in uses:
                uses[tname] = 0
                first.setdefault(o["i"], []).append(tname)
            uses[tname] += 1
    bfree = {b: (0.0, []) for b in range(8)}
    bmap, held, late = {}, {}, {}
    ready = {}
    avail = [0.0] * N_
    free = {}
    order = {}
    fin = [0.0] * N_
    for o in ops:
        if cnt[o["i"]] == 0:
            ready.setdefault(o["q"], []).append(o["i"])
    left = N_
    while left:
        best = None
        for q, lst in ready.items():
            if not lst:
                continue
            if q[0] == "R":
                cand = (avail[lst[0]], q, lst[0])
            else:
                fr = free.get(q, 0.0)
                full_ = lst
                if q == "P":
                    if not bfree:
                        lst = [i for i in lst if i not in first]
                        if not lst:
                            continue
                    else:
                        bt = min(v[0] for v in bfree.values())
                        for i in lst:
                            if i in first and avail[i] < bt:
                                late[i] = bt
                st = min(max(fr, avail[i], late.get(i, 0.0)) for i in lst)
                c = [i for i in lst if max(fr, avail[i], late.get(i, 0.0)) <= st + 0.02]
                cand = (st, q, max(c, key=lambda i: pri[i]))
            if best is None or cand[0] < best[0]:
                best = cand
        if best is None:
            pg["fin"] = 1e6
            return
        st, q, i = best
        ready[q].remove(i)
        late.clear()
        o = ops[i]
        o["dyn"] = set()
        for tname in first.get(i, ()):
            b = min(bfree, key=lambda b: bfree[b][0])
            o["dyn"] |= set(bfree.pop(b)[1])
            bmap[tname] = b
            held[tname] = [0.0, []]
        end = st + o["cost"]
        free[q] = end
        fin[i] = end + o["lat"]
        order.setdefault(q, []).append(i)
        left -= 1
        for tname in o["tiles"]:
            hd = held[tname]
            hd[0] = max(hd[0], end + WAKE)
            if q != "P":
                hd[1].append(i)
            uses[tname] -= 1
            if uses[tname] == 0:
                bfree[bmap[tname]] = (hd[0], hd[1])
        for s in succ[i]:
            cnt[s] -= 1
            w = 0.0 if i in ops[s]["ord"] else WAKE
            avail[s] = max(avail[s], fin[i] + w)
            if cnt[s] == 0:
                ready.setdefault(ops[s]["q"], []).append(s)
        o["t0"], o["t1"] = st, end
    pg["order"] = order
    pg["bmap"].clear()
    pg["bmap"].update(bmap)
    pg["fin"] = max(fin)
    pg["seq"] = sorted(range(N_), key=lambda i: (ops[i]["t0"], ops[i]["q"][0] != "R", i))


def emit(pg, g, T):
    ops = pg["ops"]
    eng = {"V": g.vector, "S": g.scalar, "P": g.tensor, "G": g, "Y": g.sync}
    pos, key, know = {}, {}, {}
    for q, lst in pg["order"].items():
        c = 0
        for i in lst:
            if ops[i]["sem"] is None:
                c += 1
                key[i], pos[i] = q, c
            else:
                key[i], pos[i] = ops[i]["sem"], ops[i]["val"]
    qk = {}
    done = {}
    queues = {q: list(l) for q, l in pg["order"].items()}
    state = {q: 0 for q in queues}
    prog = True
    tot = sum(len(l) for l in queues.values())
    k = 0
    while k < tot:
        prog = False
        for q in queues:
            while state[q] < len(queues[q]):
                i = queues[q][state[q]]
                o = ops[i]
                if o["dyn"]:
                    o["dep"] |= o["dyn"]
                if any(d not in done for d in o["dep"]) or (o["send"] is not None and o["send"] not in done):
                    break
                kn = qk.setdefault(q, {})
                if q[0] != "R":
                    need = {}
                    for d in sorted(o["dep"], key=lambda d: -ops[d]["t1"]):
                        if kn.get(key[d], 0) >= pos[d]:
                            continue
                        if need.get(key[d], 0) < pos[d]:
                            need[key[d]] = pos[d]
                    ds = [d for d in o["dep"] if need.get(key[d], 0) == pos[d]]
                    for d in ds:
                        for d2 in ds:
                            if d2 != d and key[d] in need and key[d2] in need and key[d] != key[d2] and know[d2].get(key[d], 0) >= pos[d]:
                                need.pop(key[d])
                    for kk in sorted(need):
                        eng[q].wait_ge(T.sem[kk], int(need[kk]))
                    for d in o["dep"]:
                        for kk, v in know[d].items():
                            if kn.get(kk, 0) < v:
                                kn[kk] = v
                    ins = o["fn"](eng[q])
                    if o["sem"] is None:
                        ins.then_inc(T.sem[q], 1)
                me = dict(kn)
                if o["send"] is not None:
                    me = dict(know[o["send"]])
                    for kk in list(me):
                        me.pop(kk)
                me[key[i]] = max(me.get(key[i], 0), pos[i])
                know[i] = me
                done[i] = 1
                state[q] += 1
                k += 1
                prog = True
        if not prog:
            raise ValueError("no order")
    for q in "VSPG":
        if pg["order"].get(q):
            c = sum(1 for i in pg["order"][q] if ops[i]["sem"] is None)
            if c:
                g.wait_ge(T.sem[q], int(c))


def build(T, topo, core, rank):
    pg = new_prog()
    def ap(r):
        name, c0, c1, step, p0, p1, ps = r
        t = T["b%d" % pg["bmap"][name]] if name in pg["bmap"] else T[name]
        rows = slice(p0, p1) if ps == 1 else slice(p0, p1, ps)
        cols = slice(c0, c1) if step == 1 else slice(c0, c1, step)
        return t[rows, cols]

    def cnt(r):
        return (r[2] - r[1] + r[3] - 1) // r[3]

    def two(*rs):
        return all(r[0] in SCRATCH and SCRATCH[r[0]][2] in (b2, h2, u2) for r in rs)

    def inap(x):
        if x[0] == "ind":
            return ap(x[1]).indirect(ap(x[2]))
        return ap(x)

    def regs(x):
        return [x[1], x[2]] if x[0] == "ind" else [x]

    def dcol(s):
        return ap(s) if isinstance(s, tuple) else s

    def vcost(e, c, ind):
        return FIX["V"] + CY * max(64, e * (GC if ind else c)) + (0.03 if ind else 0)

    def ts(out, in0, s1, op0, s2=None, op1=None):
        ind = in0[0] == "ind"
        sc = [s for s in (s1, s2) if isinstance(s, tuple)]
        c = 0.5 if (not ind and two(out, in0)) else 1
        if op1 is None:
            fn = lambda e: e.tensor_scalar(ap(out), inap(in0), dcol(s1), None, op0)
        else:
            fn = lambda e: e.tensor_scalar(ap(out), inap(in0), dcol(s1), dcol(s2), op0, op1)
        return add(pg, "V", vcost(cnt(out), c, ind), fn, regs(in0) + sc, [out], tag="ts " + out[0])

    def tt(out, a, b, op):
        ind = a[0] == "ind"
        ps = any(r[0][0] == "b" and r[0][1:].isdigit() for r in (a, b) if r[0] != "ind")
        return add(pg, "V", vcost(cnt(out), 1 if ps else 2, ind), lambda e: e.tensor_tensor(ap(out), inap(a), ap(b), op), regs(a) + [b], [out], tag="tt " + out[0])

    def cp(out, a):
        ind = a[0] == "ind"
        return add(pg, "V", vcost(cnt(out), 0.5 if (not ind and two(out, a)) else 1, ind), lambda e: e.tensor_copy(ap(out), inap(a)), regs(a), [out], tag="cp " + out[0])

    def scan(out, d0, d1, init, op0, op1):
        return add(pg, "V", vcost(cnt(out), 0.5 if two(out, d0, d1) else 1, False), lambda e: e.tensor_tensor_scan(ap(out), ap(d0), ap(d1), init, op0, op1), [d0, d1], [out], tag="scan " + out[0])

    def fill(out, c):
        return add(pg, "V", vcost(cnt(out), 0.5 if two(out) else 1, False), lambda e: e.memset(ap(out), c), [], [out], tag="fill " + out[0])

    def act(out, in_, func, bias=0.0, scale=1.0):
        ind = in_[0] == "ind"
        sc = [s for s in (bias, scale) if isinstance(s, tuple)]
        return add(pg, "S", FIX["S"] + CY * max(64, cnt(out) * (GC if ind else 1)) + (0.04 if ind else 0),
                   lambda e: e.activation(ap(out), inap(in_), func, bias=dcol(bias), scale=dcol(scale)), regs(in_) + sc, [out], tag="act " + out[0])

    def pe(mms):
        cost = 0.0
        rd, wr = {}, {}
        for out, l, r, s, e_ in mms:
            k = 4 if SCRATCH[l[0]][2] == f4 else 1
            cost += PEC * k * max(min(64, cnt(l)), cnt(r)) + 0.006
            for x in (l, r):
                y = rd.get(x[0])
                rd[x[0]] = (x[0], min(x[1], y[1]) if y else x[1], max(x[2], y[2]) if y else x[2], 1, 0, 128, 1)
            y = wr.get(out[0])
            wr[out[0]] = (out[0], min(out[1], y[1]) if y else out[1], max(out[2], y[2]) if y else out[2], 1, 0, 128, 1)

        def fn(e):
            ins = None
            for out, l, r, s, e_ in mms:
                ins = e.matmul(ap(out), ap(l), ap(r), s, e_)
            return ins
        return add(pg, "P", cost + FIX["P"], fn, list(rd.values()), list(wr.values()), tag="pe " + mms[0][0][0])

    def acc(out, *pairs):
        return [(out, l, r, i == 0, i == len(pairs) - 1) for i, (l, r) in enumerate(pairs)]

    def bank(h, w=n):
        pg["rr"][0] += 1
        return "b%d" % (99 + pg["rr"][0])

    def load(name, out, src, q="Y"):
        s = "ld_" + name
        return add(pg, q, 0.1, lambda e: e.dma_start(ap(out), src).then_inc(T.sem[s], 16), [], [out], sem=s, val=16, lat=3.0, tag="load " + name)

    nout = [0]

    def store(dst, in_, q="Y"):
        nout[0] += 16
        return add(pg, q, 0.1, lambda e: e.dma_start(dst, ap(in_)).then_inc(T.sem["out"], 16), [in_], [], sem="out", val=nout[0], lat=2.5, tag="store")

    dst = T.cores[(rank + 1) % 4]
    rid, pid, _se = topo.addr(dst)
    mask = sum(1 << e for e in topo.engines(core, dst))
    neng = len(topo.engines(core, dst))
    nls = [0]

    def send(kind, t, h, out, in_):
        s = "r%s_%d_%d" % (kind, t, h)
        nls[0] += neng
        i = add(pg, "G", 0.4, lambda e: e.remote_dma(ap(out), ap(in_), T.sem[s], T.sem["ls"], pid, rid, mask), [in_], [], sem="ls", val=nls[0], lat=LNK, tag="send " + s)
        j = add(pg, "R" + s, 0.0, None, [], [out], sem=s, val=neng)
        pg["ops"][j]["send"] = i

    sm = lambda name, h, w=8, x=0, k=8: ref(name, h * w + x, h * w + x + k)
    tl = lambda name, h: ref(name, h * n, h * n + n)
    full = lambda name: ref(name, 0, SCRATCH[name][1][1])

    load("wt", ref("WT", 0, 1), T.wt[:, :])
    load("kap", ref("WT", 1, 2), T.kap[:, :])
    fill(full("VZ"), 0)
    load("v0", ref("VZ", 0, 256, 1, 0, 128, 16), T.v0[:, :])
    load("d0", ref("VZ", 256, 512, 1, 0, 128, 16), T.d0[:, :])
    load("px0", ref("PX", 0, 2048), T.px[:, 0:2048])
    load("px1", ref("PX", 2048, 4096), T.px[:, 2048:4096])
    for h in (1, 0):
        load("z%d" % h, ref("XZ", h * XW + 32, h * XW + 32 + n), T.z0[:, h * n:h * n + n])
    load("f0", full("FI"), T.f0[:, :])
    load("vw0", ref("VW", 0, 1024), T.vw[:, 0:1024])
    load("vw1", ref("VW", 1024, 2048), T.vw[:, 1024:2048])

    def sel(out, in_, pat, cmp, fillv, base, cm):
        return add(pg, "G", 0.2 + 2 * CY * cnt(out), lambda e: e.affine_select(ap(out), ap(in_), pat, cmp, fillv, base, cm), [in_], [out], tag="sel")

    def iota(out, pat, base, cm, small=False):
        if small:
            fn = lambda e: e.iota(ap(out), pat, base, cm, allow_small_or_imprecise_dtypes=True)
        else:
            fn = lambda e: e.iota(ap(out), pat, base, cm)
        return add(pg, "G", 0.2 + 2 * CY * cnt(out), fn, [], [out], tag="iota")

    iota0 = lambda out: iota(out, [[0, cnt(out)]], 0, 0, True)
    fill(full("ONE"), 1.0)
    sel(full("G8"), full("ONE"), [[1, 128]], A.is_ge, 0.0, 0, -16)
    sel(full("G8"), full("G8"), [[-1, 128]], A.is_ge, 0.0, 15, 16)
    sel(full("If"), full("ONE"), [[-1, 128]], A.is_equal, 0.0, 0, 1)
    iota(ref("PI", 0, 1), [[0, 1]], 0, 1)
    iota(full("IJ"), [[1, 16]], 0, 0, True)
    iota(full("CMI"), [[16, 8]], 0, 0, True)
    iota(full("KC"), [[0, 8], [1, 16]], 0, 0, True)
    g8 = ref("G8", 0, 128, 1, 0, 8)
    bk = bank(0)
    pe([(ref(bk, 0, 128), g8, g8, True, True)])
    cp(full("BO"), ref(bk, 0, 128))
    cp(full("BOh"), full("BO"))
    cp(full("Ib"), full("If"))
    cp(full("Ih"), full("If"))
    act(full("Inb"), full("If"), F.Copy, 0.0, -1.0)
    act(full("Ihalf"), full("If"), F.Copy, 0.0, 0.5)
    act(full("I16b"), full("If"), F.Copy, 0.0, 16.0)
    ts(ref("PI", 16, 17), ref("PI", 0, 1), 15, A.bitwise_and)
    ts(ref("PI", 24, 25), ref("PI", 0, 1), 1, A.bitwise_and)
    pm, sg, sgn, pmh = ref("PC", 0, 1), ref("PC", 4, 5), ref("PC", 8, 9), ref("PC", 12, 13)
    ts(sgn, ref("PI", 24, 25), -2.0, A.mult, 1.0 + n, A.add)
    ts(pmh, ref("PI", 16, 17), -7.5, A.add)
    cp(pm, ref("PI", 16, 17))
    ts(sg, ref("PI", 24, 25), -2.0, A.mult, 1.0, A.add)
    cp(ref("WTf", 0, 2), full("WT"))
    wcol, kcol = ref("WTf", 0, 1), ref("WTf", 1, 2)
    act(full("WB"), full("BO"), F.Copy, 0.0, wcol)
    fill(full("Bh"), 0.0)
    cp(ref("Bh", 15, 143, 16), ref("BO", 0, 128, 16))
    fill(full("CLB"), -65536.0)
    HB = ref("CLB", 0, 1)
    act(full("WBs"), full("WB"), F.Copy, 0.0, 1.0 / 4096)
    act(full("I4kn"), full("If"), F.Copy, 0.0, -4096.0)
    fill(ref("CH", 0, 128, 1, 0, 64), -0.5 / 64)
    fill(ref("CH", 0, 128, 1, 64, 128), 2.0 ** -19)
    ts(full("B32"), ref("BO", 0, 128, 16), 32.0, A.mult)
    ts(full("Bm16"), ref("BO", 0, 128, 16), -16.0, A.mult)
    ts(full("OJ"), full("IJ"), pm, A.is_equal, 613.0, A.mult)
    ts(full("OK"), full("IJ"), pm, A.is_equal)
    for j in range(16):
        ts(ref("SJ", 128 * j, 128 * j + 128), full("BOh"), ref("OJ", j, j + 1), A.mult)
    for j in range(16):
        act(ref("SJb", 128 * j, 128 * j + 128), full("BO"), F.Copy, 0.0, ref("OK", j, j + 1))
    ts(ref("CM", 0, 8), full("CMI"), pm, A.add)
    ts(ref("CM", 8, 16), full("CMI"), pm, A.add)
    ts(ref("CM", 16, 24), ref("CM", 0, 8), float(2 * n), A.add)
    ts(ref("CM", 24, 32), ref("CM", 0, 8), float(3 * n), A.add)
    iota(ref("CON", 56, 72), [[0, 16]], -100, 0, True)
    for h in range(2):
        ts(sm("CMm", h), ref("CM", 0, 8), float(n * h), A.add)
    consts = (-9, -4096, 2048, -100, 1, 100)
    for i, c in enumerate(consts):
        iota(ref("CON", 8 * i, 8 * i + 8), [[0, 8]], c, 0, True)
    con = lambda c: ref("CON", 8 * consts.index(int(c)), 8 * consts.index(int(c)) + 8)
    ts(full("BO613"), full("BOh"), 613.0, A.mult)
    for nm, c in (("In", float(n)), ("I2n", float(2 * n)), ("I8k", 8192.0), ("Im100", -100.0), ("Ip100", 100.0), ("I8kn", -8192.0), ("Imh", -0.5), ("I7h", 7.5)):
        act(full(nm), full("If"), F.Copy, 0.0, c)
    act(full("G0"), full("If"), F.Copy, 0.0, sg)
    act(full("Gn"), full("If"), F.Copy, 0.0, sgn)
    act(full("BP"), ref("BO", 0, 128, 16), F.Copy, 0.0, -1048576.0)
    act(ref("Sb", 0, 128, 2), ref("If", 1, 128, 2), F.Copy)
    act(ref("Sb", 1, 128, 2), ref("If", 0, 128, 2), F.Copy)
    act(full("Sb100"), full("Sb"), F.Copy, 0.0, 100.0)
    act(full("I4k"), full("If"), F.Copy, 0.0, 4096.0)
    fill(full("ON"), 1.0)
    fill(full("CQ"), -0.25 / 128)
    iota(full("MK"), [[0, 16 * n]], 1, 0, True)
    sel(full("MK"), full("MK"), [[0, n], [1, 16]], A.not_equal, 0.0, 0, 0)
    iota(full("MF"), [[0, n]], 1, 0, True)
    sel(full("MF"), full("MF"), [[0, n // 16], [1, 16]], A.not_equal, 0.0, 0, 0)
    iota(full("RST"), [[0, 128]], 0, 0, True)
    sel(full("RST"), full("RST"), [[0, 8], [1, 16]], A.not_equal, 1048576.0, 0, 0)
    fill(full("QS"), 0.0)
    fill(full("C256"), 256.0)
    iota(full("VS"), [[0, 2 * n]], 0, 0, True)
    iota(full("SP"), [[0, 2 * n]], 0, 0, True)
    for k in range(8):
        iota0(ref("ZB", k * (32 + n) + 24, k * (32 + n) + 32))

    def ots(out, tile, base="Bh", first=(), last=()):
        prs = list(first)
        for j in range(16):
            prs.append((ref(base, 15 - j, 143 - j), ref(tile[0], tile[1] + j, tile[2], 16)))
        return acc(out, *(prs + list(last)))

    def spread(out, src):
        return [(ref(out[0], out[1] + j, out[2], 16), ref("SJ", 128 * j, 128 * j + 128), src, True, True) for j in range(16)]

    ts(ref("VZi", 0, 256), ref("VZ", 0, 256), 4032, A.bitwise_and)
    cp(ref("VZh", 0, 256), ref("VZi", 0, 256))
    ts(ref("VZi", 256, 512), ref("VZ", 0, 256), 63, A.bitwise_and)
    cp(ref("VZh", 256, 512), ref("VZi", 256, 512))
    cp(ref("VZh", 512, 768), ref("VZ", 256, 512))

    def s16(c0):
        return [(ref("Bh", 15 - j, 143 - j), ref("VZh", c0 + j, c0 + 256, 16)) for j in range(16)]
    b6, b5 = bank(0), bank(0)
    pe(acc(ref(b6, 0, 16), *(s16(0) + s16(256))))
    pe(acc(ref(b5, 0, 16), *s16(512)))
    for h in (1, 0):
        ts(ref("VH", 8 * h, 8 * h + 8), ref(b6, 8 * h, 8 * h + 8), -2048.0, A.add)
        fill(ref("XZ", h * XW, h * XW + 16), 0.0)
        ts(ref("XZ", h * XW + 16, h * XW + 24), ref(b5, 8 * h, 8 * h + 8), 1.0, A.add)
        cp(ref("W", h * WW + n, h * WW + 2 * n), ref("FI", h * n, h * n + n))
    for c in range(2):
        x = ref("VW", 1024 * c, 1024 * c + 1024)
        it = ref("IT", 1024 * c, 1024 * c + 1024)
        ts(it, x, 4095, A.bitwise_and)
        cp(ref("VI", 1024 * c, 1024 * c + 1024), it)
        ts(x, x, 12, A.arith_shift_right)
        cp(ref("VI", 2048 + 1024 * c, 3072 + 1024 * c), x)

    def tiles(t, h):
        k = 2 * t + h
        x0, w0 = k * XW, k * WW
        return {"cnt": lambda j: ref("XZ", x0 + 8 * j, x0 + 8 * j + 8), "z": ref("XZ", x0 + 32, x0 + 32 + n), "x": ref("XZ", x0 + 32 + n, x0 + 32 + 2 * n),
                "hz": ref("XZ", x0 + 32 + 2 * n, x0 + 32 + 3 * n), "xz": ref("XZ", x0 + 32, x0 + 32 + 2 * n), "xzh": ref("XZ", x0 + 32, x0 + 32 + 3 * n),
                "hd": ref("W", w0, w0 + n), "f": ref("W", w0 + n, w0 + 2 * n), "e": ref("W", w0 + 2 * n, w0 + 3 * n), "c": ref("W", w0 + 3 * n, w0 + 4 * n),
                "w2": ref("W", w0, w0 + 2 * n), "w3": ref("W", w0, w0 + 3 * n), "w4": ref("W", w0, w0 + 4 * n), "vh": ref("VH", 8 * k, 8 * k + 8),
                "land": ref("XZ", x0, x0 + 32 + n), "zb": ref("ZB", k * (32 + n), (k + 1) * (32 + n)), "zf": ref("ZB", k * (32 + n) + 32, (k + 1) * (32 + n)),
                "zc": ref("ZB", k * (32 + n), k * (32 + n) + 24), "fb": ref("FB", k * n, k * n + n), "vb": ref("VB", 8 * k, 8 * k + 8)}

    px, views = full("PX"), ref("VI", 0, 4096)
    vks = {}

    def mark(name, h):
        pg["st"] = name + str(h)

    def front(t, h):
        mark("fr", h)
        L = tiles(t, h)
        otl = sm("OTL", h)
        ts(otl, L["vh"], 2048.0, A.add)
        act(L["x"], ("ind", px, otl), F.Copy)
        act(L["e"], ("ind", views, otl), F.Copy)
        bk = bank(h)
        vk = ref(bank(h), 0, n)
        vks[h] = vk
        dx = ref(bk, 0, n)
        pe(acc(dx, (full("Ib"), L["x"]), (full("Inb"), L["z"])))
        y = ref(bank(h), 0, n)
        pe(acc(y, (full("WBs"), L["z"]), (full("CH"), full("ON"))))
        act(tl("AB", h), dx, F.Abs)
        ts(tl("IND", h), tl("AB", h), 72.0, A.is_le)
        pe([(vk, full("BO613"), full("C256"), True, False)]
           + [(ref(vk[0], j, n, 16), ref("SJ", 128 * j, 128 * j + 128), L["vh"], False, j == 15) for j in range(16)])
        ct = ref(bank(h), 0, 8)
        pe(ots(ct, tl("IND", h), "Bh", [(full("Ib"), con(-9.0))], [(full("Inb"), L["cnt"](1))]))
        lk = sm("LK", h)
        ts(lk, ct, -0.5, A.is_ge)
        b = bank(h)
        pe([(ref(b, 0, 16), full("Ih"), ref("CM", 0, 16), True, False), (ref(b, 0, 8), full("In"), lk, False, False), (ref(b, 8, 16), full("I2n"), lk, False, True)]
           + acc(ref(b, 16, 24), (full("Ih"), L["vh"]), (full("Ib"), con(-4096.0)), (full("I8k"), lk)))
        cp(sm("LSL", h, 16, 0, 16), ref(b, 0, 16))
        act(ref("VS", h * n, h * n + n, 16), ref(b, 16, 24), F.Relu, 0.0, 613.0)
        q0 = h * 16 * n
        mark("qx", h)
        ts(ref("QS", 0, 16 * n, 16), ("ind", L["xz"], sm("LSL", h, 16)), -512.0, A.add)
        scan(ref("QX", q0, q0 + 16 * n), full("MK"), full("QS"), 0.0, A.mult, A.add)
        a, c = tl("HI1", h), tl("HI2", h)
        mark("ha", h)
        act(tl("T2", h), y, F.Identity, MAGIC)
        act(tl("FL", h), tl("T2", h), F.Identity, -MAGIC)
        um = ref(y[0], n, 2 * n)
        pe(acc(um, (full("WB"), L["z"]), (full("I4kn"), tl("FL", h))))
        act(tl("T2", h), um, F.Identity, HB, kcol)
        cp(a, tl("T2", h))
        ts(c, a, 5, A.arith_shift_right)
        tt(a, c, vk, A.add)
        ts(c, a, 4095, A.bitwise_and)
        cp(L["hd"], c)
        mark("dd", h)
        scan(tl("VR", h), full("MF"), tl("VS", h), 0.0, A.mult, A.add)
        tt(tl("EQ", h), tl("VR", h), vk, A.is_equal)
        tt(ref("EQ2", h * n + 16, h * n + n), ref("VR", h * n, h * n + n - 16), ref(vk[0], 16, n), A.is_equal)
        for i in range(2):
            mark("he"[i], h)
            he = ref("HE", (2 * h + i) * n, (2 * h + i + 1) * n)
            act(he, ("ind", L["w2"] if i == 0 else L["w3"], sm("LSL", h, 16, 8 * i)), F.Copy)
            cp(ref("HEL", (2 * h + i) * n, (2 * h + i + 1) * n), he)

    def dedupe(t, h):
        mark("dd", h)
        L = tiles(t, h)
        lk = sm("LK", h)
        du = ref(bank(h), 0, 8)
        m3 = acc(du, *([(full("Ib"), con(100.0)), (full("Im100"), lk)] + [(ref("LTJ", 128 * j, 128 * j + 128), ref("EQ", h * n + j, h * n + n, 16)) for j in range(16)]))
        m3[-1] = m3[-1][:4] + (False,)
        pe(m3 + [(ref(du[0], 1, 8, 2), ref("Bh", 15 - j, 143 - j), ref("EQ2", h * n + 16 + j, h * n + n, 32), False, j == 15) for j in range(16)])
        ts(sm("W0", h), du, 0.5, A.is_lt)
        vd = ref(bank(h), 0, 8)
        pe(acc(vd, (full("Ib"), con(2048.0)), (full("Ih"), sm("CMm", h)), (full("I8kn"), sm("W0", h))))
        tt(sm("O2", h), L["vh"], vd, A.max)
        ts(sm("OFF", h), sm("O2", h), 2048.0, A.add)

    def early(t, h):
        mark("ea", h)
        L = tiles(t, h)
        lk, d1, ov = sm("LK", h), sm("D1", h), sm("OV", h)
        Ih, Ib, Sb, Ip, Im = full("Ih"), full("Ib"), full("Sb"), full("Ip100"), full("Im100")
        hz = ref(bank(h), 0, n)
        pe(acc(hz, (full("Ihalf"), L["x"]), (full("Ihalf"), L["z"]), (full("CQ"), full("ON"))))
        act(tl("T1", h), hz, F.Identity, MAGIC)
        act(L["hz"], tl("T1", h), F.Identity, -MAGIC)
        dp = ref(bank(h), 0, 8)
        pe(acc(dp, (Ib, L["cnt"](2)), (Im, lk)))
        act(d1, dp, F.Relu)
        po = ref(bank(h), 0, 8)
        pe(acc(po, (Ib, d1), (full("Sb100"), lk)))
        ts(ov, po, 101.5, A.is_ge)
        b = bank(h)
        pe([(ref(b, 0, 24), Ih, ref("CM", 8, 32), True, False)]
           + [(ref(b, c, c + 8), full(m), v, False, c == 16) for c, m, v in ((0, "I2n", lk), (0, "I2n", ov), (0, "G0", ov), (8, "In", lk), (8, "Gn", ov), (16, "G0", ov))])
        cp(sm("TLL", h, 24, 0, 24), ref(b, 0, 24))
        act(L["zf"], ("ind", L["xzh"], sm("TLL", h, 24)), F.Copy)
        b = bank(h)
        pe([(ref(b, 0, 16), Ib, ref(L["cnt"](0)[0], L["cnt"](0)[1], L["cnt"](1)[2]), True, False), (ref(b, 0, 8), Ib, lk, False, False), (ref(b, 8, 16), full("Inb"), lk, False, True)])
        ap_ = sm("P1", h, 16, 0, 16)
        act(ap_, ref(b, 0, 16), F.Abs)
        act(sm("O2V", h, 16), ov, F.Copy)
        act(sm("O2V", h, 16, 8), ov, F.Copy)
        oo = sm("O2V", h, 16, 0, 16)
        b = bank(h)
        pe(acc(ref(b, 0, 16), (Ib, ap_), (Im, oo)) + acc(ref(b, 16, 32), (Sb, ap_), (Ip, oo), (Ib, ref("CON", 56, 72))) + acc(ref(b, 32, 40), (Ib, d1), (Im, ov)))
        ra = lambda j: sm("RA", h, 40, 8 * j)
        ra2 = lambda j: sm("RA", h, 40, 16 * j, 16)
        act(sm("RA", h, 40, 0, 40), ref(b, 0, 40), F.Relu)
        b = bank(h)
        if t < NT - 1:
            pe(acc(ref(b, 0, 16), (Ib, ra2(0)), (Ib, ra2(1))) + acc(ref(b, 16, 24), (Ib, ra(4)), (Ib, con(1.0))))
            act(L["zc"], ref(b, 0, 24), F.Copy)
            send("z", t + 1, h, tiles(t + 1, h)["land"], L["zb"])
        else:
            i16 = full("I16b")
            pe(acc(ref(b, 0, 8), (i16, ra(0)), (i16, ra(2)), (Ib, ra(4))))
            act(sm("YC", h), ref(b, 0, 8), F.Copy)
            b = ref(bank(h), 0, n)
            pe([(ref(b[0], j, n, 16), ref("SJb", 128 * j, 128 * j + 128), sm("YC", h), True, True) for j in range(16)])
            act(ref("YU", h * n, h * n + n), b, F.Copy)
            store(T.yc[:, h * n:h * n + n], ref("YU", h * n, h * n + n, 1, 0, 128, 16))
            act(ref("YU", 1024 + h * n, 1024 + h * n + n), L["zf"], F.Copy)
            store(T.yz[:, h * n:h * n + n], ref("YU", 1024 + h * n, 1024 + h * n + n))
        mark("kk", h)
        cb = ref(bank(h), 0, 8)
        pe(acc(cb, (full("Imh"), lk), (full("I7h"), ov)))
        act(sm("CB", h), cb, F.Identity, t - 7.0)
        y = ref(bank(h), 0, n)
        pe([(y, full("BO"), L["zf"], True, False)]
           + [(ref(y[0], j, n, 16), ref("SJb", 128 * j, 128 * j + 128), sm("CB", h), False, j == 15) for j in range(16)])
        act(tl("KT", h), y, F.Identity, MAGIC, 1.0 / 16)
        act(tl("KU", h), tl("KT", h), F.Identity, -MAGIC)
        act(tl("KT", h), tl("KU", h), F.Identity, pmh, 16.0)
        tt(tl("OHL", h), tl("KT", h), y, A.is_equal)

    def bulk(t, h):
        mark("hb", h)
        L = tiles(t, h)
        q0, e0 = h * 16 * n, h * 2 * n
        key = tl("KEY", h)
        bh_, be_ = bank(h), bank(h)

        def part(G, D, R, l0, a, b, fused):
            g_, d_, r_ = ref(G, q0 + 16 * a, q0 + 16 * b), ref(D, q0 + 16 * a, q0 + 16 * b), ref(R, q0 + 16 * a, q0 + 16 * b)
            off = ref("HEL", l0 + a, l0 + b)
            qx = ref("QX", q0 + 16 * a, q0 + 16 * b)
            if fused:
                tt(d_, ("ind", px, off), qx, A.subtract)
            else:
                act(g_, ("ind", px, off), F.Copy)
                scan(d_, g_, qx, 600.0, A.min, A.subtract)
            ts(r_, d_, 512.0, A.max)

        def sums(out, D, R, first):
            mm = []
            if first:
                mm.append((out, full("Ib"), full("KC"), True, False))
            for k in range(16):
                o = ref(out[0], out[1] + k, out[2], 16)
                mm.append((o, ref(R, q0 + k, q0 + 16 * n, 16), full("B32"), not first, False))
                mm.append((o, ref(D, q0 + k, q0 + 16 * n, 16), full("Bm16"), False, (not first) or k == 15))
            if len(mm) > 30:
                pe(mm[:17])
                pe(mm[17:])
            else:
                pe(mm)
        ph, pd = ref(bh_, 0, n), ref(be_, 0, n)
        part("GH", "DH", "RH", e0, 0, n // 2, False)
        part("GH", "DH", "RH", e0, n // 2, n, False)
        sums(ph, "DH", "RH", True)
        act(key, ph, F.Copy)
        he1, he2 = ref("HE", e0, e0 + n), ref("HE", e0 + n, e0 + 2 * n)
        mark("hm", h)
        tt(tl("HME", h), he1, he2, A.subtract)
        mark("km", h)
        scan(tl("PM", h), full("RST"), key, 0.0, A.add, A.min)
        mx = ref(bank(h), 0, 8)
        pe([(mx, tl("OHL", h), full("BP"), True, True)])
        tt(ref("SP", h * n, h * n + n, 16), ref("PM", h * n + 15, h * n + n, 16), mx, A.add)
        scan(tl("MN", h), full("MF"), tl("SP", h), 0.0, A.mult, A.add)
        tt(tl("OHT", h), tl("MN", h), ph, A.is_equal)
        mark("eb", h)
        if NE > 0:
            part("GE", "DE", "RE", e0 + n, 0, NE, False)
        if NE < n:
            part("GE", "DE", "RE", e0 + n, NE, n, True)
        sums(pd, "DE", "RE", False)
        mark("cc", h)
        tt(tl("MT", h), key, pd, A.is_lt)
        mk = ref(bank(h), 0, n)
        pe([(mk, tl("MT", h), full("Ib"), True, True)])
        tt(tl("MM", h), tl("HME", h), mk, A.mult)
        tt(L["c"], tl("MM", h), he2, A.add)
        act(tl("CF", h), ("ind", L["w4"], sm("TLL", h, 24, 16)), F.Identity, -2048.0)
        oc = ref(bank(h), 0, n)
        pe([(oc, tl("OHT", h), full("Ib"), True, False), (oc, full("Ib"), tl("OHL", h), False, True)])
        tt(tl("PP", h), tl("CF", h), oc, A.mult)
        vo = ref(bank(h), 0, n)
        if t < NT - 1:
            vo = ref(vo[0], 0, 8)
            pe(ots(vo, tl("PP", h)))
            cp(L["vb"], vo)
            send("v", t + 1, h, tiles(t + 1, h)["vh"], L["vb"])
        else:
            pe(acc(vo, (full("BOh"), tl("PP", h))))
            act(ref("YU", 512 + h * n, 512 + h * n + n), vo, F.Identity, 2048.0)
            store(T.yv[:, h * n:h * n + n], ref("YU", 512 + h * n, 512 + h * n + n, 1, 0, 128, 16))
        mark("ff", h)
        act(L["fb"], ("ind", L["w4"], sm("TLL", h, 24, 8)), F.Copy)
        if t < NT - 1:
            send("f", t + 1, h, tiles(t + 1, h)["f"], L["fb"])
        else:
            store(T.yf[:, h * n:h * n + n], L["fb"])

    def scatter(t, h):
        mark("sc", h)
        L = tiles(t, h)
        c0 = L["c"][1]
        for c in range(3, -1, -1):
            add(pg, "V", 0.18, lambda e, c=c: e.tensor_copy(ap(full("VI")).indirect(ap(ref("OFF", h * 8 + 2 * c, h * 8 + 2 * c + 2))), ap(ref("W", c0 + 32 * c, c0 + 32 * c + 32))),
                [ref("OFF", h * 8 + 2 * c, h * 8 + 2 * c + 2), ref("W", c0 + 32 * c, c0 + 32 * c + 32)], [full("VI")], tag="scatter")

    front(0, 1)
    sel(full("BOg"), full("BO"), [[1, 128]], A.is_gt, 0.0, 0, -1)
    iota(full("LTJ"), [[0, 2048]], 0, 0, True)
    for j in range(16):
        act(ref("LTJ", 128 * j + j, 128 * j + 128, 16), ref("BOg", j, 128, 16), F.Copy)
    fill(ref("VI", 4096, 4096 + 2 * n), 0.0)
    front(0, 0)
    for t in range(NT):
        for h in (1, 0):
            if t > 0 and h == 1:
                pass
            early(t, h)
            dedupe(t, h)
            bulk(t, h)
            scatter(t, h)
            if t < NT - 1 and h == 1:
                pass
        if t < NT - 1:
            front(t + 1, 1)
            front(t + 1, 0)
    pg["st"] = ""
    for c in (3, 0, 1, 2):
        a, b = 512 * c, 512 * c + 512
        if c == 3:
            yb = ref(bank(0), 0, 512)
            pe(acc(yb, (full("If"), ref("VI", a, b)), (full("I4k"), ref("VI", 2048 + a, 2048 + b))))
            act(ref("YT", a, b), yb, F.Copy)
            store(T.yw[:, a:b], ref("YT", a, b))
            continue
        act(ref("YT", a, b), ref("VI", 2048 + a, 2048 + b), F.Copy, 0.0, 4096.0)
        tt(ref("YT", a, b), ref("YT", a, b), ref("VI", a, b), A.add)
        store(T.yw[:, a:b], ref("YT", a, b))
    pg["nls"], pg["nout"] = nls[0], nout[0]
    return pg


def rank_program(g, core, T, topo):
    rank = T.rank_of(core)
    if rank is None:
        return
    pg = build(T, topo, core, rank)
    schedule(pg)
    emit(pg, g, T)
    g.wait_ge(T.sem["ls"], int(pg["nls"]))
    g.wait_ge(T.sem["out"], int(pg["nout"]))
